import numpy as np, ml_dtypes
CORES = [3,7,11,15,131,135,139,143]
N = 8
import mx_ref
BF = ml_dtypes.bfloat16
def gcols(t, e):
    v = np.concatenate([t.reshape(8, 16, -1, 4), np.zeros((8, 16, 1, 4), BF)], axis=2)
    return np.ascontiguousarray(np.stack([v[g][:, e[g]] for g in range(8)])).reshape(128, -1)
def tile(rs):
    return np.stack(rs, axis=2).reshape(128, -1).astype(BF)
def cut(t, i, w=512):
    return t[:, w * i:w * i + w]
def pick(q, e):
    c = np.concatenate([q[0].reshape(128, -1, 4), np.zeros((128, 1, 4), np.uint8)], axis=1); s = np.concatenate([q[1], np.ones((16, 1), np.uint8)], axis=1)
    return (np.ascontiguousarray(c[:, e].reshape(128, -1)), np.ascontiguousarray(s[:, e]))
def join(*qs):
    return (np.concatenate([q[0] for q in qs], axis=1), np.concatenate([q[1] for q in qs], axis=1))
def put(q, e, v):
    c, s = q[0].reshape(128, -1, 4).copy(), q[1].copy(); c[:, e] = v[0].reshape(128, -1, 4); s[:, e] = v[1]
    return (c.reshape(128, -1), s)
def pk(c, s):
    return (np.ascontiguousarray(c), mx_ref.live(s))
def emit(q):
    return q[0], q[1]
def packed(v, rng):
    q = [mx_ref.quantize(np.ascontiguousarray(v[r])) for r in range(N)]
    return np.stack([a for a, b in q]), np.stack([mx_ref.plane(b, rng) for a, b in q])
def values_of_codes():
    e, c = np.zeros((128, 128, 4), np.float32), np.zeros((128, 2, 4), np.uint8)
    e[np.arange(128), np.arange(128), 0] = 1
    c[:127, :, 0] = np.arange(256).reshape(2, 128).T[:127]
    return mx_ref.matmul(mx_ref.quantize(e.reshape(128, 512).astype(BF)), (c.reshape(128, 8), np.full((16, 2), 127, np.uint8))).T.reshape(-1).astype(np.float64)
CODE_VALUE, SCALE_VALUE = values_of_codes(), 2.0 ** (np.arange(256) - 127.0)
def decode(q):
    return (CODE_VALUE[q[0]].reshape(16, 8, -1, 4) * SCALE_VALUE[q[1]][:, None, :, None] + 0.0).reshape(128, -1).astype(np.float32)
def f(rng, *shape):
    return mx_ref.flush((rng.standard_normal(shape, dtype=np.float32) * np.exp2(rng.integers(-2, 3, shape[:-1] + (1,)))).astype(BF))
def wide(rng, *shape, cols=0):
    v = rng.standard_normal(shape, dtype=np.float32) * np.exp2(rng.integers(-12, 13, shape)).astype(np.float32)
    if cols: v *= np.repeat(np.exp2(rng.integers(-cols, cols + 1, shape[:-2] + (1, shape[-1] // 4))) * (rng.random(shape[:-2] + (1, shape[-1] // 4)) > 0.0625), 4, axis=-1).astype(np.float32)
    return mx_ref.flush(v.astype(BF))
C, L, M, R = 352, 128, 224, 3
STEP = [1, 2, 4]
def order(p):
    return np.argsort(-(p[::16] + np.float32(0.0)), axis=1, kind="stable")
def numbers_of(rng):
    return {"x": np.array(f(rng, N, 128, 4 * C)), "u": np.array(f(rng, N, 128, 512)), "v": np.array(f(rng, N, 128, 512))}
def weights(rng, still=[]):
    w = np.array(f(rng, N, 128, 2048)).reshape(N, 8, 16, 4, 8, 16, 4)
    for i in still:
        w[:, :, i] = 0
        w[:, :, :, :, :, i] = 0
    c, p = packed(w.reshape(N, 128, 2048), rng)
    return {"wc": c, "ws": p}
def signs(rng):
    return np.stack([rng.permutation(8) % 2 * 2.0 - 1.0 for r in range(N)])
def setup_inputs(rng):
    return {**numbers_of(rng), **weights(rng)}
def setup_inputs_ties(rng):
    d = numbers_of(rng)
    e = rng.permutation(N)
    x = d["x"].reshape(N, 8, 16, C, 4)
    for r in range(N):
        k = np.zeros(C, int) if r == e[0] else rng.permutation(C) % 3
        a = x[r][:, :8, :3].copy()
        a[:, :, 2] = 0
        x[r][:, :8] = a[:, :, k]
    x[e[1]] = 0
    u = d["u"].reshape(N, 8, 16, 8, 16, 4)
    k = u.copy()
    u[:, :, :, :, :2] = 0
    for g in range(8): u[:, g, :8, g, :2] = k[:, g, :8, g, :2]
    return {"x": x.reshape(N, 128, 4 * C), "u": u.reshape(N, 128, 512), "v": d["v"], **weights(rng, range(8))}
def setup_inputs_near(rng):
    d = numbers_of(rng)
    x = d["x"].astype(np.float32).reshape(N, 8, 16, C, 4)
    s = np.arange(C) // 2
    g = ((s[:, None] >> np.arange(8)) & 1) * np.exp2(np.arange(8) - 23.0)
    x[:, :, 0] = 0
    x[:, :, 0, :, 0] = signs(rng)[:, :, None]
    for r in range(N):
        for i in rng.permutation(8)[:4]: x[r, i, 0, rng.integers(C), 0] *= np.float32(2.0 ** 30)
    x[:, :, 8] = g[:, :4]
    x[:, :, 9] = g[:, 4:]
    x[:, :, 10:] = rng.integers(4, 8, (N, 8, 6, C, 4)) * rng.choice([-1.0, 1.0], (N, 8, 6, C, 4)) * 2.0 ** -20
    u = d["u"].reshape(N, 128, 128, 4)
    k = np.where(rng.permutation(N) < N // 2, 2.0 ** -30, 1.0).astype(np.float32).astype(BF)
    u[:, :, ::16] = 0
    for h in range(0, 128, 16):
        u[:, h, h, 0] = k
        u[:, h + 8:h + 10, h] = k[:, None, None]
    return {"x": x.reshape(N, 128, 4 * C).astype(BF), "u": u.reshape(N, 128, 512), "v": d["v"], **weights(rng, [0, 8, 9, 10, 11, 12, 13, 14, 15])}
def setup_inputs_starts(rng):
    d = numbers_of(rng)
    x = d["x"].astype(np.float32).reshape(N, 8, 16, C, 4)
    u = d["u"].reshape(N, 128, 128, 4)
    size = np.where(rng.permutation(N) < N // 2, 2.0 ** -30, 1.0).astype(np.float32)
    x[:, :, :11] = 0
    n = np.stack([rng.permutation([0, 1, M // 2, M - 1, M, M + 1, C - 1, C]) for r in range(N)])
    o = np.argsort(rng.random((N, 8, C)), axis=2)
    for r in range(N):
        k = rng.permutation(8)
        for g in range(8):
            x[r, g, 0, :, 0] = np.where(rng.permutation(C) < n[r, g], 1, -rng.integers(0, 2, C)) * size[r]
            if r % 2 == 0:
                a, s = o[r, g], min(int(n[r, g]), M)
                seg, rest = rng.permutation(a[s:s + L]), np.concatenate([a[:s], a[s + L:]])
                if k[g] == 0: o[r ^ 1, g] = a
                if k[g] == 1: o[r ^ 1, g] = a[::-1]
                if k[g] == 2: o[r ^ 1, g] = np.concatenate([seg, rest])
                if k[g] == 3: o[r ^ 1, g] = np.concatenate([rest, seg])
    key = C - 1 - np.argsort(o, axis=2)
    z = ((key[:, :, :, None] >> np.arange(12)) & 1) * np.exp2(np.arange(12.0))
    for i in range(3): x[:, :, 8 + i] = z[:, :, :, 4 * i:4 * i + 4]
    k = size.astype(BF)
    u[:, :, ::16] = 0
    u[:, :, 1::16] = 0
    for h in range(0, 128, 16):
        u[:, h + 8:h + 11, h] = k[:, None, None]
        u[:, h, h + 1, 0] = k
    return {"x": x.reshape(N, 128, 4 * C).astype(BF), "u": u.reshape(N, 128, 512), "v": d["v"], **weights(rng, range(11))}
def setup_inputs_huge(rng):
    d = numbers_of(rng)
    x = 2.0 ** 30 * (0.8 + 0.2 * rng.random((N, 128, C, 4)))
    c = np.ones((N, C))
    half = int(rng.integers(2))
    for r in range(N):
        if 2 * r // N == half: c[r] = rng.permutation(C) % 2 * 2.0 - 1.0
    x *= c[:, None, :, None]
    u = d["u"].reshape(N, 128, 8, 16, 4)
    a = 2.0 ** 30 * (1 - 0.1 * rng.random((N, 128, 8, 2, 4))) * np.stack([signs(rng), signs(rng)], axis=2)[:, None, :, :, None]
    u[:, :, :, :2] = a.astype(np.float32).astype(BF)
    w = np.zeros((N, 128, 4, 128, 4), np.float32)
    i = np.arange(128)
    for b in range(4): w[:, i, b, i, b] = -1
    wc, ws = packed(w.reshape(N, 128, 2048).astype(BF), rng)
    return {"x": x.astype(np.float32).reshape(N, 128, 4 * C).astype(BF), "u": u.reshape(N, 128, 512), "v": d["v"], "wc": wc, "ws": ws}
def setup_inputs_spread(rng):
    d = setup_inputs(rng)
    d["x"] = wide(rng, N, 128, 4 * C, cols=6)
    return d
def check_inputs(d):
    b = []
    for k in ("x", "u", "v"):
        a = np.abs(d[k].astype(np.float32))
        if not (np.isfinite(a).all() and ((a == 0) | (a >= 2.0 ** -30) & (a <= 2.0 ** 30)).all()): b.append("a value of " + k)
    if ((d["wc"] & 0x7F) == 0x7F).any(): b.append("a code of wc that is no number")
    z = np.zeros((128, 4, 4), np.float32)
    z[:, 1] = 2.0 ** -30
    z[:, 2] = 2.0 ** 30
    c, s = emit(mx_ref.quantize(z.reshape(128, 16).astype(BF)))
    for r in range(N):
        p = mx_ref.live(d["ws"][r])
        if not ((p == s[0, 0]) | (p >= s[0, 1]) & (p <= s[0, 2])).all(): b.append("a scale of ws")
    return b
def reference(x, u, v, wc, ws):
    qu = [mx_ref.quantize(u[r]) for r in range(N)]
    lay = [pk(wc[r], ws[r]) for r in range(N)]
    now = [x[r] for r in range(N)]
    place = np.arange(C)
    for t in range(R):
        sent, o, start = [], [], []
        for r in range(N):
            q = mx_ref.quantize(now[r])
            p = mx_ref.matmul(qu[r], q)
            sent.append(q)
            o.append(order(p))
            start.append(np.minimum(np.sum(p[1::16] > 0, axis=1), M)[:, None])
        came = decode(join(*sent)).astype(BF)
        made, child = [], []
        for r in range(N):
            e = r ^ STEP[t]
            own = (place >= start[r]) & (place < start[r] + L)
            h = o[r].copy()
            for g in range(8): h[g, ~own[g]] = o[e][g][~np.isin(o[e][g], o[r][g][own[g]])]
            c = gcols(np.concatenate([now[r], cut(came, e, 4 * C)], axis=1), np.where(own, h, C + h))
            q = mx_ref.quantize(c)
            made.append(tile([mx_ref.matmul(pick(lay[r], np.arange(128 * b, 128 * b + 128)), q) * np.float32(0.015625) + c[:, b::4].astype(np.float32) for b in range(4)]))
            child.append(h)
        now = made
    y, ot = np.zeros((N, 128, C), np.float32), np.zeros((N, 8, C), np.float32)
    oc, osc = np.zeros((N, 128, 4 * C), np.uint8), np.zeros((N, 16, C), np.uint8)
    for r in range(N):
        q = mx_ref.quantize(now[r])
        y[r] = mx_ref.matmul(mx_ref.quantize(v[r]), q)
        ot[r] = child[r]
        oc[r], osc[r] = emit(q)
    return {"y": y, "ot": ot, "oc": oc, "osc": osc}

@@ -1,0 +1,324 @@
+from concourse.mybir import dt, AluOpType, ActivationFunctionType
+
+C = 352
+ROUNDS = 3
+SLOTS = [(352, [0, 21, 20, 19]), (288, [18, 17, 16, 15]), (224, [14, 13, 12, 11]), (160, [10, 9, 8, 7]),
+         (128, [6, 5, 4, 3]), (128, [2, 1])]
+
+SCRATCH = {}
+
+
+def _add(where, dtype, **names):
+    for n, w in names.items():
+        SCRATCH[n] = (where, [128, w], dtype)
+
+
+F8 = "float8_e4m3fn_x4"
+_add("sbuf", "bfloat16", UB=512, VB=512, TD0=8 * C, TD1=8 * C, TD2=8 * C, TD3=4 * C, FT=4 * C, F64=4 * C,
+     EBA=2048, WBA=1024, JUNK=8 * 22 * 21)
+_add("sbuf", F8, UQ=128, UU=256, VQ=128, WQ=512, FQ=C, EQA=512, WQA=256, GQA=1280)
+_add("sbuf", "uint8", US=128, UV=256, VS=128, WP=512, FS=C, ESA=512, WSA=256, GSA=1280)
+PART = {}
+for _i in range(4):
+    PART["EB%d" % _i], PART["EQ%d" % _i], PART["ES%d" % _i] = ("EBA", 512 * _i, 512), ("EQA", 128 * _i, 128), ("ESA", 128 * _i, 128)
+    PART["AC%d" % _i], PART["ET%d" % _i] = ("ACA", C * _i, C), ("ETA", 512 * _i, 512)
+for _i in range(2):
+    PART["W%dB" % (_i + 1)], PART["W%dQ" % (_i + 1)], PART["W%dS" % (_i + 1)] = \
+        ("WBA", 512 * _i, 512), ("WQA", 128 * _i, 128), ("WSA", 128 * _i, 128)
+for _t in range(ROUNDS + 1):
+    _add("sbuf", F8, **{"TQ%d" % _t: C})
+    _add("sbuf", "uint8", **{"TS%d" % _t: C})
+for _t in range(ROUNDS):
+    _add("sbuf", F8, **{"RQ%d" % _t: C})
+    _add("sbuf", "uint8", **{"RP%d" % _t: C})
+    _add("sbuf", "uint16", **{"LO%d" % _t: 22, "LR%d" % _t: 22})
+for _m, (_w, _k) in enumerate(SLOTS):
+    _add("sbuf", "bfloat16", **{"G%d" % _m: 4 * _w})
+    for _n in ("GQ", "GS"):
+        PART["%s%d" % (_n, _m)] = (_n + "A", sum(w for w, k in SLOTS[:_m]), _w)
+_add("sbuf", "uint16", OFU=16, DST=22, L2=88)
+_add("sbuf", "int32", IU=16, PI=2, KI=4)
+_add("sbuf", "float32", C16=C, C4=C, M512=512, BD=512, CWI=22, NPB=4, N4=C, NV=C, Q5=C, KF=4, COL=8,
+     NE16=C, NE4=C, MK=C, D0=C, RST=C, PKA=C, PKB=C, CW=22, ETA=2048,
+     DM=C, PX=C, DS=C, RS=22, TA=22, TB=22, PKX=C, RF=22, SGN=C, SGP=C, NC=2, WC1=2, BC=2, SC=2,
+     SQ=C, SG2=C, SEG=C, NSEG=C, RKT=C, RKR=C, NKR=C, KP=C, E1=C, GX=C, GP=C, MM=22, DD=22,
+     HW=992, HP=C, ACA=4 * C, YB=C, HQ=C, HS=C, HT=C, HO=C)
+for _n in ("PB", "NB", "CS", "RB0", "RB1", "RB2", "RB3"):
+    SCRATCH[_n] = ("psum", [128, 512], "float32")
+
+SEMAPHORES = ["cv", "cs", "cp", "cg", "lx", "lu", "lv", "lwc", "lws", "sent", "od", "ot1"] + \
+    ["ad%d" % t for t in range(ROUNDS)] + ["al%d" % t for t in range(ROUNDS)]
+PSUM = {"PB", "NB", "CS", "RB0", "RB1", "RB2", "RB3"}
+
+
+def rank_program(g, core, T, topo):
+    rank = T.rank_of(core)
+    if rank is None:
+        return
+    A, AF = AluOpType, ActivationFunctionType
+    eng = {"v": g.vector, "s": g.scalar, "p": g.tensor, "g": g, "y": g.sync}
+    count = {"v": 0, "s": 0, "p": 0, "g": 0}
+    seen = {q: {} for q in eng}
+    wrote, reads_of = {}, {}
+
+    def need(q, toks):
+        toks = sorted(toks, key=lambda k: -sum(k[2].values()))
+        for sem, val, past in toks:
+            if seen[q].get(sem, 0) >= val:
+                continue
+            eng[q].wait_ge(T.sem[sem], val)
+            seen[q][sem] = val
+            for s, v in past.items():
+                seen[q][s] = max(seen[q].get(s, 0), v)
+
+    def before(q, rd, wr):
+        toks = []
+        for k in rd:
+            if k in wrote:
+                toks.append(wrote[k][1])
+            if k in PSUM:
+                toks += [tk for o, tk in reads_of.get(k, {}).items() if o != q]
+        for k in wr:
+            if k in wrote and not (q == "p" and wrote[k][0] == "p"):
+                toks.append(wrote[k][1])
+            toks += list(reads_of.get(k, {}).values())
+        need(q, toks)
+
+    def after(q, tok, rd, wr):
+        for k in rd:
+            reads_of.setdefault(k, {})[q] = tok
+        for k in wr:
+            wrote[k] = (q, tok)
+            reads_of[k] = {}
+
+    def op(q, fn, rd, wr):
+        before(q, rd, wr)
+        count[q] += 1
+        tok = ("c" + q, count[q], dict(seen[q]))
+        fn().then_inc(T.sem["c" + q], 1)
+        after(q, tok, rd, wr)
+
+    def dma(q, out, in_, sem, val, rd, wr):
+        before(q, rd, wr)
+        eng[q].dma_start(out, in_).then_inc(T.sem[sem], 16)
+        after("d" + sem, (sem, val, dict(seen[q])), rd, wr)
+
+    def B(name, a=0, b=None, step=1):
+        buf, at, n = PART.get(name) or (name, 0, SCRATCH[name][1][1])
+        return T[buf][:, at + a:at + (n if b is None else b):step]
+
+    V, S, P = g.vector, g.scalar, g.tensor
+
+    def ts(out, in0, s1, s2, o0, o1, rd, wr):
+        if o1 is None:
+            op("v", lambda: V.tensor_scalar(out, in0, s1, None, o0), rd, wr)
+        else:
+            op("v", lambda: V.tensor_scalar(out, in0, s1, s2, o0, o1), rd, wr)
+
+    def tt(out, a, b, o, rd, wr):
+        op("v", lambda: V.tensor_tensor(out, a, b, o), rd, wr)
+
+    def cp(out, a, rd, wr):
+        op("v", lambda: V.tensor_copy(out, a), rd, wr)
+
+    def scan(out, d0, d1, init, o0, o1, rd, wr):
+        op("v", lambda: V.tensor_tensor_scan(out, d0, d1, init, o0, o1), rd, wr)
+
+    def quant(c, s, tile, n, rd):
+        op("v", lambda: V.quantize_mx(B(c, 0, n), B(s, 0, n), B(tile, 0, 4 * n)), rd, [c])
+
+    def act(out, in_, f, rd, wr, **kw):
+        op("s", lambda: S.activation(out, in_, f, **kw), rd, wr)
+
+    def mm(bank, n, a, asc, b, bsc, first, last, rd):
+        op("p", lambda: P.matmul_mx(B(bank, 0, n), a, asc, b, bsc, first, last), rd, [bank])
+
+    dma("y", B("TD0", 0, 4 * C), T.x[:, :], "lx", 16, [], ["TD0x%d" % b for b in range(4)])
+    dma("s", B("UB"), T.u[:, :], "lu", 16, [], ["UB"])
+    dma("y", B("WQ").bitcast(dt.uint8), T.wc[:, :], "lwc", 16, [], ["WQ"])
+    dma("y", B("WP"), T.ws[:, :], "lws", 16, [], ["WP"])
+    dma("y", B("VB"), T.v[:, :], "lv", 16, [], ["VB"])
+
+    def iota(name, pattern, base, cm, flag=True):
+        n = 1
+        for s, k in pattern:
+            n *= k
+        if flag:
+            op("g", lambda: g.iota(B(name, 0, n), pattern, base, cm, allow_small_or_imprecise_dtypes=True), [], [name])
+        else:
+            op("g", lambda: g.iota(B(name, 0, n), pattern, base, cm), [], [name])
+
+    iota("IU", [[1, 2], [16, 8]], 0, 0, False)
+    iota("PI", [[0, 2]], 0, 1, False)
+    iota("C16", [[0, 22], [1, 16]], 0, 0)
+    iota("NPB", [[-1, 4]], 0, -4)
+    iota("CWI", [[-16, 22]], 351, 0)
+    iota("M512", [[1, 512]], 0, 0)
+    iota("BD", [[1, 8], [0, 64]], 0, 0)
+    cp(B("OFU"), B("IU"), ["IU"], ["OFU"])
+    ts(B("KI", 0, 1), B("PI", 0, 1), 15, None, A.bitwise_and, None, ["PI"], ["KI0"])
+    ts(B("KI", 1, 2), B("PI", 0, 1), 4, None, A.arith_shift_right, None, ["PI"], ["KI1"])
+    ts(B("KI", 2, 3), B("PI", 0, 1), 15, 2, A.bitwise_and, A.arith_shift_right, ["PI"], ["KI2"])
+    ts(B("KI", 3, 4), B("PI", 0, 1), 3, None, A.bitwise_and, None, ["PI"], ["KI3"])
+    cp(B("KF"), B("KI"), ["KI0", "KI1", "KI2", "KI3"], ["KF"])
+    ci, cg, cq, cr = [B("KF", j, j + 1) for j in range(4)]
+    ts(B("NE16"), B("C16"), ci, None, A.not_equal, None, ["C16", "KF"], ["NE16"])
+    for j, (m, a) in enumerate([(-1024.0, 15360.0 + 224.0), (1024.0, -15361.0), (-1025.0, 15360.0), (4096.0, -12288.0)]):
+        ts(B("COL", j, j + 1), cq if j == 3 else ci, m, a, A.mult, A.add, ["KF"], ["COL%d" % j])
+    tt(B("COL", 4, 5), B("COL", 3, 4), cr, A.add, ["COL3", "KF"], ["COL4"])
+    ts(B("CW"), B("CWI"), B("COL", 2, 3), None, A.add, None, ["CWI", "COL2"], ["CW"])
+    op("v", lambda: V.memset(B("RS", 0, 2), 0.0), [], ["RS0", "RS1"])
+    for m, (w, ks) in enumerate(SLOTS):
+        lo = 0 if len(ks) < 4 else 16 * ks[-1]
+        op("v", (lambda m=m, w=w, lo=lo: V.memset(B("G%d" % m, 4 * lo, 4 * w), 0.0)), [], ["G%d.%d" % (m, b) for b in range(4)])
+    act(B("D0"), B("C16"), AF.Copy, ["C16"], ["D0"], bias=-0.5e29, scale=1e29)
+    act(B("RST"), B("C16"), AF.Sign, ["C16"], ["RST"])
+    act(B("MK"), B("NE16"), AF.Copy, ["NE16"], ["MK"], scale=-1e29)
+    act(B("PKA"), B("NE16"), AF.Copy, ["NE16"], ["PKA"], bias=-262144.0, scale=262144.0 + 1024.0)
+    quant("UQ", "US", "UB", 128, ["UB"])
+    op("v", lambda: V.tensor_copy(B("UU").bitcast(dt.uint32), B("UQ").bitcast(dt.uint32).indirect(B("OFU"))), ["UQ", "OFU"], ["UU"])
+    op("v", lambda: V.tensor_copy(B("UV"), B("US").indirect(B("OFU"))), ["UQ", "OFU"], ["UV"])
+    for b in range(4):
+        act(B("ET%d" % b), B("M512"), AF.Abs, ["M512", "NPB"], ["ET%d" % b], bias=B("NPB", b, b + 1))
+    for b in range(4):
+        act(B("EB%d" % b), B("ET%d" % b), AF.Relu, ["ET%d" % b], ["EB%d" % b], bias=1.0, scale=-1.0)
+
+    partners = [T.cores[rank ^ (1 << t)] for t in range(ROUNDS)]
+    mask = topo.mask(core, partners[0])
+    for d in partners:
+        mask &= topo.mask(core, d)
+    ne = bin(mask).count("1")
+    sent = [0]
+
+    def send(t, out, in_, sem, val, rd, wr):
+        before("g", rd, [])
+        rid, pid = topo.addr(partners[t], core)
+        g.remote_dma(out, in_, T.sem[sem], T.sem.sent, pid, rid, mask)
+        sent[0] += ne
+        for k in wr:
+            wrote[k] = ("r", (sem, val, {}))
+
+    for t in range(ROUNDS):
+        X, tq, tsc, lo, lr, rq, rp = ["%s%d" % (n, t) for n in ("TD", "TQ", "TS", "LO", "LR", "RQ", "RP")]
+        xk = [X + "x%d" % b for b in range(4)]
+        dk = [X + "d%d" % b for b in range(4)]
+        quant(tq, tsc, X, C, xk)
+        send(t, B(rq).bitcast(dt.uint8), B(tq).bitcast(dt.uint8), "ad%d" % t, 2 * ne, [tq], [rq])
+        send(t, B(rp), B(tsc), "ad%d" % t, 2 * ne, [tq], [rp])
+        mm("PB", C, B("UU", 0, 128), B("UV", 0, 128), B(tq), B(tsc), True, True, ["UU", "UV", tq])
+        mm("NB", C, B("UU", 128, 256), B("UV", 128, 256), B(tq), B(tsc), True, True, ["UU", "UV", tq])
+        if t == 0:
+            iota("N4", [[4, C]], 0, 0)
+            iota("NV", [[4, C]], 4 * C, 0)
+            iota("C4", [[0, 88], [1, 4]], 0, 0)
+            iota("Q5", [[1, C]], 512, 0)
+            for n in ("W1B", "W2B"):
+                ts(B(n), B("BD"), cg, None, A.is_equal, None, ["BD", "KF"], [n])
+            ts(B("W2B", 0, 512, 4), B("BD", 0, 512, 4), cg, -1.0, A.is_equal, A.mult, ["BD", "KF"], ["W2B"])
+            quant("W1Q", "W1S", "W1B", 128, ["W1B"])
+            quant("W2Q", "W2S", "W2B", 128, ["W2B"])
+        act(B("SGN"), B("NB", 0, C), AF.Sign, ["NB"], ["SGN"])
+        act(B("SGP"), B("SGN"), AF.Relu, ["SGN"], ["SGP", "NC"], accum_out=B("NC", 0, 1))
+        act(B("WC1", 0, 1), B("NC", 0, 1), AF.Relu, ["NC"], ["WC1"], bias=224.0, scale=-1.0)
+        act(B("BC", 0, 1), B("WC1", 0, 1), AF.Copy, ["WC1"], ["BC"], bias=-287.5)
+        act(B("SC", 0, 1), B("WC1", 0, 1), AF.Identity, ["WC1", "COL0"], ["SC"], bias=B("COL", 0, 1), scale=-1.0)
+        tt(B("DM"), B("PB", 0, C), B("MK"), A.add, ["PB", "MK"], ["DM"])
+        scan(B("PX"), B("D0"), B("DM"), -1e29, A.min, A.max, ["D0", "DM"], ["PX"])
+        queue = []
+
+        def flush(m):
+            w = SLOTS[m][0]
+            quant("GQ%d" % m, "GS%d" % m, "G%d" % m, w, ["G%d.%d" % (m, b) for b in range(4)])
+            s = "W2" if m == 0 else "W1"
+            mm("CS", w, B(s + "Q"), B(s + "S"), B("GQ%d" % m), B("GS%d" % m), m == 0, m == len(SLOTS) - 1, [s + "Q", "GQ%d" % m])
+
+        for m, (w, ks) in enumerate(SLOTS):
+            for b, k in enumerate(ks):
+                gk = "G%d.%d" % (m, b)
+                if k == 0:
+                    tt(B("G0", 0, 4 * C, 4), B("PB", 0, C), B("PX"), A.is_le, ["PB", "PX"], [gk])
+                else:
+                    n = 16 * k
+                    ts(B("G%d" % m, b, 4 * n, 4), B("PB", 0, n), B("PX", n + 15, n + 16), None, A.is_ge, None, ["PB", "PX"], [gk])
+                    act(B("JUNK", 8 * k * (k - 1), 8 * k * (k + 1)), B("G%d" % m, b, 4 * n, 4), AF.Copy, [gk], ["J%d" % k, "RS%d" % k],
+                        accum_out=B("RS", k, k + 1))
+                if b == 0 and queue:
+                    flush(queue.pop())
+                if m == 0 and b == 2:
+                    scan(B("DS"), B("RST"), B("G0", 0, 4 * C, 4), 0.0, A.mult, A.add, ["RST", "G0.0"], ["DS"])
+            queue.append(m)
+        flush(queue.pop())
+        tt(B("TA"), B("CW"), B("DS", 15, C, 16), A.subtract, ["CW", "DS"], ["TA"])
+        tt(B("TB"), B("TA"), B("RS"), A.add, ["TA"] + ["RS%d" % k for k in range(22)], ["TB"])
+        scan(B("PKX"), B("PKA"), B("CS", 0, C), 0.0, A.add, A.max, ["PKA", "CS"], ["PKX"])
+        tt(B("RF"), B("TB"), B("PKX", 15, C, 16), A.subtract, ["TB", "PKX"], ["RF"])
+        cp(B(lo), B("RF"), ["RF"], [lo])
+        send(t, B(lr), B(lo), "al%d" % t, ne, [lo], [lr])
+        act(B("SQ"), B("M512", 0, C), AF.Square, ["M512", "BC"], ["SQ"], bias=B("BC", 0, 1))
+        act(B("SG2"), B("SQ"), AF.Sign, ["SQ"], ["SG2"], bias=4096.0, scale=-1.0)
+        act(B("SEG"), B("SG2"), AF.Relu, ["SG2"], ["SEG"])
+        act(B("NSEG"), B("SG2"), AF.Relu, ["SG2"], ["NSEG"], scale=-1.0)
+        act(B("NKR"), B("NSEG").indirect(B(lo)), AF.Copy, ["NSEG", lo], ["NKR"])
+        op("v", lambda: V.tensor_copy(B("HW").indirect(B(lo)), B("N4")), ["N4", lo], ["HW"])
+        tt(B("RKT"), B("SEG"), B("Q5"), A.mult, ["SEG", "Q5"], ["RKT"])
+        cp(B("RKR"), B("RKT").indirect(B(lo)), ["RKT", lo], ["RKR"])
+        if t == 0:
+            for b in range(4):
+                quant("EQ%d" % b, "ES%d" % b, "EB%d" % b, 128, ["EB%d" % b])
+            ts(B("NE4"), B("C4"), cq, None, A.not_equal, None, ["C4", "KF"], ["NE4"])
+            act(B("PKB"), B("NE4"), AF.Copy, ["NE4"], ["PKB"], bias=-262144.0, scale=262144.0 + 4096.0)
+            quant("VQ", "VS", "VB", 128, ["VB"])
+        for b in range(4):
+            mm("RB%d" % b, C, B("EQ%d" % b), B("ES%d" % b), B(rq), B(rp), True, True, ["EQ%d" % b, rq, rp])
+        for b in range(4):
+            act(B(X, 4 * C + b, 8 * C, 4), B("RB%d" % b, 0, C), AF.Copy, ["RB%d" % b], [dk[b]])
+        op("v", lambda: V.tensor_copy(B("KP").indirect(B(lr)), B("NKR")), ["NKR", lr], ["KP"])
+        scan(B("E1"), B("KP"), B("KP"), 0.0, A.add, A.max, ["KP"], ["E1"])
+        tt(B("GX"), B("E1").indirect(B(lr)), B("RKR"), A.max, ["E1", lr, "RKR"], ["GX"])
+        scan(B("GP"), B("PKA"), B("GX"), 0.0, A.add, A.max, ["PKA", "GX"], ["GP"])
+        gp = B("GP", 15, C, 16)
+        ts(B("MM"), gp, B("SC", 0, 1), 128.0, A.is_gt, A.mult, ["GP", "SC"], ["MM"])
+        tt(B("DD"), gp, B("MM"), A.add, ["GP", "MM"], ["DD"])
+        ts(B("DST"), B("DD"), B("COL", 1, 2), None, A.add, None, ["DD", "COL1"], ["DST"])
+        op("v", lambda: V.tensor_copy(B("HW").indirect(B("DST")), B("NV")), ["NV", "DST"], ["HW"])
+        scan(B("HP"), B("PKB"), B("HW", 0, C), 0.0, A.add, A.max, ["PKB", "HW"], ["HP"])
+        ts(B("L2"), B("HP", 3, C, 4), B("COL", 4, 5), None, A.add, None, ["HP", "COL4"], ["L2"])
+        if t == ROUNDS - 1:
+            act(B("HQ"), B("HW", 0, C), AF.Copy, ["HW"], ["HQ"], bias=-176.0, scale=0.25)
+            act(B("HS"), B("HW", 0, C), AF.Sign, ["HW", "HM"], ["HS"], bias=-1407.0)
+        half = 2 * C
+        cp(B("FT", 0, half), B(X).indirect(B("L2", 0, 44)), xk + dk + ["L2"], ["FTa"])
+        act(B("FT", half, 4 * C), B(X).indirect(B("L2", 44, 88)), AF.Copy, xk + dk + ["L2"], ["FTb"])
+        quant("FQ", "FS", "FT", C, ["FTa", "FTb"])
+        for b in (2, 3):
+            act(B("F64", b, 4 * C, 4), B("FT", b, 4 * C, 4), AF.Copy, ["FTa", "FTb"], ["F64%d" % b], scale=64.0)
+        for b in (0, 1):
+            ts(B("F64", b, 4 * C, 4), B("FT", b, 4 * C, 4), 64.0, None, A.mult, None, ["FTa", "FTb"], ["F64%d" % b])
+        Y = "TD%d" % (t + 1)
+        for b in range(4):
+            mm("RB%d" % b, C, B("WQ", 128 * b, 128 * b + 128), B("WP", 128 * b, 128 * b + 128), B("FQ"), B("FS"), True, True, ["WQ", "WP", "FQ"])
+            tt(B("AC%d" % b), B("RB%d" % b, 0, C), B("F64", b, 4 * C, 4), A.add, ["RB%d" % b, "F64%d" % b], ["AC%d" % b])
+            act(B(Y, b, 4 * C, 4), B("AC%d" % b), AF.Copy, ["AC%d" % b], [Y + "x%d" % b], scale=0.015625)
+
+    quant("TQ3", "TS3", "TD3", C, ["TD3x%d" % b for b in range(4)])
+    mm("PB", C, B("VQ"), B("VS"), B("TQ3"), B("TS3"), True, True, ["VQ", "TQ3"])
+    act(B("HT"), B("HS"), AF.Copy, ["HS"], ["HT"], scale=-176.0)
+    stores = []
+
+    def store(q, out, in_, rd):
+        before(q, rd, [])
+        stores.append("od" if q == "y" else "ot1")
+        eng[q].dma_start(out, in_).then_inc(T.sem[stores[-1]], 16)
+
+    store("y", T.oc[:, :], B("TQ3").bitcast(dt.uint8), ["TQ3"])
+    for k in range(4):
+        store("y", T.osc[4 * k:4 * k + 4, :], T.TS3[32 * k:32 * k + 4, :], ["TQ3"])
+    act(B("YB"), B("PB", 0, C), AF.Copy, ["PB"], ["YB"])
+    tt(B("HO"), B("HQ"), B("HT"), A.add, ["HQ", "HT"], ["HO"])
+    store("y", T.y[:, :], B("YB"), ["YB"])
+    store("s", T.ot[:, :], T.HO[0:128:16, :], ["HO"])
+    g.wait_ge(T.sem.sent, sent[0])
+    for q in ("v", "s", "p", "g"):
+        g.wait_ge(T.sem["c" + q], count[q])
+    g.wait_ge(T.sem.od, 16 * stores.count("od"))
+    g.wait_ge(T.sem.ot1, 16 * stores.count("ot1"))

@@ -1,6 +1,7 @@
 from concourse.mybir import dt, AluOpType, ActivationFunctionType
 
 C = 352
+H = C // 2
 ROUNDS = 3
 SLOTS = [(352, [0, 21, 20, 19]), (288, [18, 17, 16, 15]), (224, [14, 13, 12, 11]), (160, [10, 9, 8, 7]),
          (128, [6, 5, 4, 3]), (128, [2, 1])]
@@ -15,16 +16,13 @@ def _add(where, dtype, **names):
 
 F8 = "float8_e4m3fn_x4"
 _add("sbuf", "bfloat16", UB=512, VB=512, TD0=8 * C, TD1=8 * C, TD2=8 * C, TD3=4 * C, FT=4 * C, F64=4 * C,
-     EBA=2048, WBA=1024, JUNK=8 * 22 * 21)
-_add("sbuf", F8, UQ=128, UU=256, VQ=128, WQ=512, FQ=C, EQA=512, WQA=256, GQA=1280)
-_add("sbuf", "uint8", US=128, UV=256, VS=128, WP=512, FS=C, ESA=512, WSA=256, GSA=1280)
+     EBA=2048, W1B=512, JUNK=8 * 22 * 21)
+_add("sbuf", F8, UQ=128, UU=256, VQ=128, WQ=512, FQ=C, EQA=512, W1Q=128, GQA=1280)
+_add("sbuf", "uint8", US=128, UV=256, VS=128, WP=512, FS=C, ESA=512, W1S=128, GSA=1280)
 PART = {}
 for _i in range(4):
     PART["EB%d" % _i], PART["EQ%d" % _i], PART["ES%d" % _i] = ("EBA", 512 * _i, 512), ("EQA", 128 * _i, 128), ("ESA", 128 * _i, 128)
     PART["AC%d" % _i], PART["ET%d" % _i] = ("ACA", C * _i, C), ("ETA", 512 * _i, 512)
-for _i in range(2):
-    PART["W%dB" % (_i + 1)], PART["W%dQ" % (_i + 1)], PART["W%dS" % (_i + 1)] = \
-        ("WBA", 512 * _i, 512), ("WQA", 128 * _i, 128), ("WSA", 128 * _i, 128)
 for _t in range(ROUNDS + 1):
     _add("sbuf", F8, **{"TQ%d" % _t: C})
     _add("sbuf", "uint8", **{"TS%d" % _t: C})
@@ -41,14 +39,15 @@ _add("sbuf", "int32", IU=16, PI=2, KI=4)
 _add("sbuf", "float32", C16=C, C4=C, M512=512, BD=512, CWI=22, NPB=4, N4=C, NV=C, Q5=C, KF=4, COL=8,
      NE16=C, NE4=C, MK=C, D0=C, RST=C, PKA=C, PKB=C, CW=22, ETA=2048,
      DM=C, PX=C, DS=C, RS=22, TA=22, TB=22, PKX=C, RF=22, SGN=C, SGP=C, NC=2, WC1=2, BC=2, SC=2,
-     SQ=C, SG2=C, SEG=C, NSEG=C, RKT=C, RKR=C, NKR=C, KP=C, E1=C, GX=C, GP=C, MM=22, DD=22,
+     SQ=C, SG2=C, SEG=C, NSEG=C, RKR=C, NKR=C, KP=C, E1=C, GX=C, GP=C, MM=22, DD=22,
      HW=992, HP=C, ACA=4 * C, YB=C, HQ=C, HS=C, HT=C, HO=C)
-for _n in ("PB", "NB", "CS", "RB0", "RB1", "RB2", "RB3"):
+PSUM = ["PB", "NB", "CS", "RB0", "RB1", "RB2", "RB3", "RB4"]
+HALF = [["RB0", "RB1", "RB2", "RB3"], ["RB4", "NB", "CS", "PB"]]
+for _n in PSUM:
     SCRATCH[_n] = ("psum", [128, 512], "float32")
 
-SEMAPHORES = ["cv", "cs", "cp", "cg", "lx", "lu", "lv", "lwc", "lws", "sent", "od", "ot1"] + \
+SEMAPHORES = ["cv", "cs", "cp", "cg", "lx0", "lx1", "lu", "lv", "lwc", "lws", "sent", "od", "os"] + \
     ["ad%d" % t for t in range(ROUNDS)] + ["al%d" % t for t in range(ROUNDS)]
-PSUM = {"PB", "NB", "CS", "RB0", "RB1", "RB2", "RB3"}
 
 
 def rank_program(g, core, T, topo):
@@ -101,7 +100,7 @@ def rank_program(g, core, T, topo):
     def dma(q, out, in_, sem, val, rd, wr):
         before(q, rd, wr)
         eng[q].dma_start(out, in_).then_inc(T.sem[sem], 16)
-        after("d" + sem, (sem, val, dict(seen[q])), rd, wr)
+        after("d" + sem, (sem, val, dict(seen[q])), [], wr)
 
     def B(name, a=0, b=None, step=1):
         buf, at, n = PART.get(name) or (name, 0, SCRATCH[name][1][1])
@@ -124,8 +123,8 @@ def rank_program(g, core, T, topo):
     def scan(out, d0, d1, init, o0, o1, rd, wr):
         op("v", lambda: V.tensor_tensor_scan(out, d0, d1, init, o0, o1), rd, wr)
 
-    def quant(c, s, tile, n, rd):
-        op("v", lambda: V.quantize_mx(B(c, 0, n), B(s, 0, n), B(tile, 0, 4 * n)), rd, [c])
+    def quant(c, s, tile, n, rd, a=0, key=None):
+        op("v", lambda: V.quantize_mx(B(c, a, a + n), B(s, a, a + n), B(tile, 4 * a, 4 * (a + n))), rd, [key or c])
 
     def act(out, in_, f, rd, wr, **kw):
         op("s", lambda: S.activation(out, in_, f, **kw), rd, wr)
@@ -133,11 +132,12 @@ def rank_program(g, core, T, topo):
     def mm(bank, n, a, asc, b, bsc, first, last, rd):
         op("p", lambda: P.matmul_mx(B(bank, 0, n), a, asc, b, bsc, first, last), rd, [bank])
 
-    dma("y", B("TD0", 0, 4 * C), T.x[:, :], "lx", 16, [], ["TD0x%d" % b for b in range(4)])
+    def xkeys(t, h):
+        return ["TD%dx%d%d" % (t, h, b) for b in range(4)]
+
     dma("s", B("UB"), T.u[:, :], "lu", 16, [], ["UB"])
-    dma("y", B("WQ").bitcast(dt.uint8), T.wc[:, :], "lwc", 16, [], ["WQ"])
-    dma("y", B("WP"), T.ws[:, :], "lws", 16, [], ["WP"])
-    dma("y", B("VB"), T.v[:, :], "lv", 16, [], ["VB"])
+    dma("y", B("TD0", 0, 4 * H), T.x[:, 0:4 * H], "lx0", 16, [], xkeys(0, 0))
+    dma("y", B("TD0", 4 * H, 4 * C), T.x[:, 4 * H:4 * C], "lx1", 16, [], xkeys(0, 1))
 
     def iota(name, pattern, base, cm, flag=True):
         n = 1
@@ -150,9 +150,9 @@ def rank_program(g, core, T, topo):
 
     iota("IU", [[1, 2], [16, 8]], 0, 0, False)
     iota("PI", [[0, 2]], 0, 1, False)
-    iota("C16", [[0, 22], [1, 16]], 0, 0)
     iota("NPB", [[-1, 4]], 0, -4)
     iota("CWI", [[-16, 22]], 351, 0)
+    iota("C16", [[0, 22], [1, 16]], 0, 0)
     iota("M512", [[1, 512]], 0, 0)
     iota("BD", [[1, 8], [0, 64]], 0, 0)
     cp(B("OFU"), B("IU"), ["IU"], ["OFU"])
@@ -165,81 +165,86 @@ def rank_program(g, core, T, topo):
     ts(B("NE16"), B("C16"), ci, None, A.not_equal, None, ["C16", "KF"], ["NE16"])
     for j, (m, a) in enumerate([(-1024.0, 15360.0 + 224.0), (1024.0, -15361.0), (-1025.0, 15360.0), (4096.0, -12288.0)]):
         ts(B("COL", j, j + 1), cq if j == 3 else ci, m, a, A.mult, A.add, ["KF"], ["COL%d" % j])
+    op("v", lambda: V.memset(B("RS", 0, 2), 0.0), [], ["RS0", "RS1"])
     tt(B("COL", 4, 5), B("COL", 3, 4), cr, A.add, ["COL3", "KF"], ["COL4"])
     ts(B("CW"), B("CWI"), B("COL", 2, 3), None, A.add, None, ["CWI", "COL2"], ["CW"])
-    op("v", lambda: V.memset(B("RS", 0, 2), 0.0), [], ["RS0", "RS1"])
     for m, (w, ks) in enumerate(SLOTS):
         lo = 0 if len(ks) < 4 else 16 * ks[-1]
         op("v", (lambda m=m, w=w, lo=lo: V.memset(B("G%d" % m, 4 * lo, 4 * w), 0.0)), [], ["G%d.%d" % (m, b) for b in range(4)])
     act(B("D0"), B("C16"), AF.Copy, ["C16"], ["D0"], bias=-0.5e29, scale=1e29)
-    act(B("RST"), B("C16"), AF.Sign, ["C16"], ["RST"])
     act(B("MK"), B("NE16"), AF.Copy, ["NE16"], ["MK"], scale=-1e29)
     act(B("PKA"), B("NE16"), AF.Copy, ["NE16"], ["PKA"], bias=-262144.0, scale=262144.0 + 1024.0)
     quant("UQ", "US", "UB", 128, ["UB"])
     op("v", lambda: V.tensor_copy(B("UU").bitcast(dt.uint32), B("UQ").bitcast(dt.uint32).indirect(B("OFU"))), ["UQ", "OFU"], ["UU"])
-    op("v", lambda: V.tensor_copy(B("UV"), B("US").indirect(B("OFU"))), ["UQ", "OFU"], ["UV"])
     for b in range(4):
         act(B("ET%d" % b), B("M512"), AF.Abs, ["M512", "NPB"], ["ET%d" % b], bias=B("NPB", b, b + 1))
+    act(B("UV"), B("US").indirect(B("OFU")), AF.Copy, ["UQ", "OFU"], ["UV"])
     for b in range(4):
         act(B("EB%d" % b), B("ET%d" % b), AF.Relu, ["ET%d" % b], ["EB%d" % b], bias=1.0, scale=-1.0)
+    act(B("RST"), B("C16"), AF.Sign, ["C16"], ["RST"])
+    ts(B("W1B"), B("BD"), cg, None, A.is_equal, None, ["BD", "KF"], ["W1B"])
+    dma("y", B("WQ").bitcast(dt.uint8), T.wc[:, :], "lwc", 16, ["UQ"], ["WQ"])
+    dma("y", B("WP"), T.ws[:, :], "lws", 16, [], ["WP"])
+    dma("y", B("VB"), T.v[:, :], "lv", 16, [], ["VB"])
 
     partners = [T.cores[rank ^ (1 << t)] for t in range(ROUNDS)]
-    mask = topo.mask(core, partners[0])
-    for d in partners:
-        mask &= topo.mask(core, d)
-    ne = bin(mask).count("1")
+    masks = [topo.mask(core, d) for d in partners]
+    ne = [len(topo.engines(core, d)) for d in partners]
     sent = [0]
 
     def send(t, out, in_, sem, val, rd, wr):
         before("g", rd, [])
         rid, pid = topo.addr(partners[t], core)
-        g.remote_dma(out, in_, T.sem[sem], T.sem.sent, pid, rid, mask)
-        sent[0] += ne
+        g.remote_dma(out, in_, T.sem[sem], T.sem.sent, pid, rid, masks[t])
+        sent[0] += ne[t]
         for k in wr:
             wrote[k] = ("r", (sem, val, {}))
 
+    def pack(t):
+        for h in range(2):
+            quant("TQ%d" % t, "TS%d" % t, "TD%d" % t, H, xkeys(t, h), H * h, "TQ%dh%d" % (t, h))
+
+    pack(0)
+    quant("W1Q", "W1S", "W1B", 128, ["W1B"])
     for t in range(ROUNDS):
         X, tq, tsc, lo, lr, rq, rp = ["%s%d" % (n, t) for n in ("TD", "TQ", "TS", "LO", "LR", "RQ", "RP")]
-        xk = [X + "x%d" % b for b in range(4)]
+        tk = [tq + "h0", tq + "h1"]
+        xk = xkeys(t, 0) + xkeys(t, 1)
         dk = [X + "d%d" % b for b in range(4)]
-        quant(tq, tsc, X, C, xk)
-        send(t, B(rq).bitcast(dt.uint8), B(tq).bitcast(dt.uint8), "ad%d" % t, 2 * ne, [tq], [rq])
-        send(t, B(rp), B(tsc), "ad%d" % t, 2 * ne, [tq], [rp])
-        mm("PB", C, B("UU", 0, 128), B("UV", 0, 128), B(tq), B(tsc), True, True, ["UU", "UV", tq])
-        mm("NB", C, B("UU", 128, 256), B("UV", 128, 256), B(tq), B(tsc), True, True, ["UU", "UV", tq])
+        send(t, B(rq).bitcast(dt.uint8), B(tq).bitcast(dt.uint8), "ad%d" % t, 2 * ne[t], tk, [rq])
+        send(t, B(rp), B(tsc), "ad%d" % t, 2 * ne[t], tk, [rp])
+        mm("RB0", H, B("UU", 0, 128), B("UV", 0, 128), B(tq, 0, H), B(tsc, 0, H), True, True, ["UU", "UV", tk[0]])
+        mm("PB", C, B("UU", 0, 128), B("UV", 0, 128), B(tq), B(tsc), True, True, ["UU", "UV"] + tk)
+        mm("NB", C, B("UU", 128, 256), B("UV", 128, 256), B(tq), B(tsc), True, True, ["UU", "UV"] + tk)
         if t == 0:
             iota("N4", [[4, C]], 0, 0)
-            iota("NV", [[4, C]], 4 * C, 0)
-            iota("C4", [[0, 88], [1, 4]], 0, 0)
             iota("Q5", [[1, C]], 512, 0)
-            for n in ("W1B", "W2B"):
-                ts(B(n), B("BD"), cg, None, A.is_equal, None, ["BD", "KF"], [n])
-            ts(B("W2B", 0, 512, 4), B("BD", 0, 512, 4), cg, -1.0, A.is_equal, A.mult, ["BD", "KF"], ["W2B"])
-            quant("W1Q", "W1S", "W1B", 128, ["W1B"])
-            quant("W2Q", "W2S", "W2B", 128, ["W2B"])
+            iota("C4", [[0, 88], [1, 4]], 0, 0)
+            iota("NV", [[4, C]], 4 * C, 0)
         act(B("SGN"), B("NB", 0, C), AF.Sign, ["NB"], ["SGN"])
         act(B("SGP"), B("SGN"), AF.Relu, ["SGN"], ["SGP", "NC"], accum_out=B("NC", 0, 1))
         act(B("WC1", 0, 1), B("NC", 0, 1), AF.Relu, ["NC"], ["WC1"], bias=224.0, scale=-1.0)
         act(B("BC", 0, 1), B("WC1", 0, 1), AF.Copy, ["WC1"], ["BC"], bias=-287.5)
         act(B("SC", 0, 1), B("WC1", 0, 1), AF.Identity, ["WC1", "COL0"], ["SC"], bias=B("COL", 0, 1), scale=-1.0)
-        tt(B("DM"), B("PB", 0, C), B("MK"), A.add, ["PB", "MK"], ["DM"])
-        scan(B("PX"), B("D0"), B("DM"), -1e29, A.min, A.max, ["D0", "DM"], ["PX"])
+        for h, bank in enumerate(("RB0", "PB")):
+            a, z = H * h, H * h + H
+            tt(B("DM", a, z), B(bank, a, z), B("MK", a, z), A.add, [bank, "MK"], ["DM%d" % h])
+            scan(B("PX", a, z), B("D0", a, z), B("DM", a, z), -1e29, A.min, A.max, ["D0", "DM%d" % h], ["PX%d" % h])
         queue = []
 
         def flush(m):
             w = SLOTS[m][0]
             quant("GQ%d" % m, "GS%d" % m, "G%d" % m, w, ["G%d.%d" % (m, b) for b in range(4)])
-            s = "W2" if m == 0 else "W1"
-            mm("CS", w, B(s + "Q"), B(s + "S"), B("GQ%d" % m), B("GS%d" % m), m == 0, m == len(SLOTS) - 1, [s + "Q", "GQ%d" % m])
+            mm("CS", w, B("W1Q"), B("W1S"), B("GQ%d" % m), B("GS%d" % m), m == 0, m == len(SLOTS) - 1, ["W1Q", "GQ%d" % m])
 
         for m, (w, ks) in enumerate(SLOTS):
             for b, k in enumerate(ks):
                 gk = "G%d.%d" % (m, b)
                 if k == 0:
-                    tt(B("G0", 0, 4 * C, 4), B("PB", 0, C), B("PX"), A.is_le, ["PB", "PX"], [gk])
+                    tt(B("G0", 0, 4 * C, 4), B("PB", 0, C), B("PX"), A.is_gt, ["PB", "PX0", "PX1"], [gk])
                 else:
                     n = 16 * k
-                    ts(B("G%d" % m, b, 4 * n, 4), B("PB", 0, n), B("PX", n + 15, n + 16), None, A.is_ge, None, ["PB", "PX"], [gk])
+                    ts(B("G%d" % m, b, 4 * n, 4), B("PB", 0, n), B("PX", n + 15, n + 16), None, A.is_ge, None, ["PB", "PX0", "PX1"], [gk])
                     act(B("JUNK", 8 * k * (k - 1), 8 * k * (k + 1)), B("G%d" % m, b, 4 * n, 4), AF.Copy, [gk], ["J%d" % k, "RS%d" % k],
                         accum_out=B("RS", k, k + 1))
                 if b == 0 and queue:
@@ -248,30 +253,30 @@ def rank_program(g, core, T, topo):
                     scan(B("DS"), B("RST"), B("G0", 0, 4 * C, 4), 0.0, A.mult, A.add, ["RST", "G0.0"], ["DS"])
             queue.append(m)
         flush(queue.pop())
-        tt(B("TA"), B("CW"), B("DS", 15, C, 16), A.subtract, ["CW", "DS"], ["TA"])
+        tt(B("TA"), B("CW"), B("DS", 15, C, 16), A.add, ["CW", "DS"], ["TA"])
         tt(B("TB"), B("TA"), B("RS"), A.add, ["TA"] + ["RS%d" % k for k in range(22)], ["TB"])
         scan(B("PKX"), B("PKA"), B("CS", 0, C), 0.0, A.add, A.max, ["PKA", "CS"], ["PKX"])
         tt(B("RF"), B("TB"), B("PKX", 15, C, 16), A.subtract, ["TB", "PKX"], ["RF"])
         cp(B(lo), B("RF"), ["RF"], [lo])
-        send(t, B(lr), B(lo), "al%d" % t, ne, [lo], [lr])
+        send(t, B(lr), B(lo), "al%d" % t, ne[t], [lo], [lr])
         act(B("SQ"), B("M512", 0, C), AF.Square, ["M512", "BC"], ["SQ"], bias=B("BC", 0, 1))
         act(B("SG2"), B("SQ"), AF.Sign, ["SQ"], ["SG2"], bias=4096.0, scale=-1.0)
-        act(B("SEG"), B("SG2"), AF.Relu, ["SG2"], ["SEG"])
         act(B("NSEG"), B("SG2"), AF.Relu, ["SG2"], ["NSEG"], scale=-1.0)
+        act(B("SEG"), B("SG2"), AF.Relu, ["SG2"], ["SEG"])
         act(B("NKR"), B("NSEG").indirect(B(lo)), AF.Copy, ["NSEG", lo], ["NKR"])
         op("v", lambda: V.tensor_copy(B("HW").indirect(B(lo)), B("N4")), ["N4", lo], ["HW"])
-        tt(B("RKT"), B("SEG"), B("Q5"), A.mult, ["SEG", "Q5"], ["RKT"])
-        cp(B("RKR"), B("RKT").indirect(B(lo)), ["RKT", lo], ["RKR"])
+        tt(B("RKR"), B("SEG").indirect(B(lo)), B("Q5"), A.mult, ["SEG", lo, "Q5"], ["RKR"])
         if t == 0:
             for b in range(4):
                 quant("EQ%d" % b, "ES%d" % b, "EB%d" % b, 128, ["EB%d" % b])
             ts(B("NE4"), B("C4"), cq, None, A.not_equal, None, ["C4", "KF"], ["NE4"])
-            act(B("PKB"), B("NE4"), AF.Copy, ["NE4"], ["PKB"], bias=-262144.0, scale=262144.0 + 4096.0)
             quant("VQ", "VS", "VB", 128, ["VB"])
         for b in range(4):
             mm("RB%d" % b, C, B("EQ%d" % b), B("ES%d" % b), B(rq), B(rp), True, True, ["EQ%d" % b, rq, rp])
         for b in range(4):
             act(B(X, 4 * C + b, 8 * C, 4), B("RB%d" % b, 0, C), AF.Copy, ["RB%d" % b], [dk[b]])
+        if t == 0:
+            act(B("PKB"), B("NE4"), AF.Copy, ["NE4"], ["PKB"], bias=-262144.0, scale=262144.0 + 4096.0)
         op("v", lambda: V.tensor_copy(B("KP").indirect(B(lr)), B("NKR")), ["NKR", lr], ["KP"])
         scan(B("E1"), B("KP"), B("KP"), 0.0, A.add, A.max, ["KP"], ["E1"])
         tt(B("GX"), B("E1").indirect(B(lr)), B("RKR"), A.max, ["E1", lr, "RKR"], ["GX"])
@@ -286,39 +291,43 @@ def rank_program(g, core, T, topo):
         if t == ROUNDS - 1:
             act(B("HQ"), B("HW", 0, C), AF.Copy, ["HW"], ["HQ"], bias=-176.0, scale=0.25)
             act(B("HS"), B("HW", 0, C), AF.Sign, ["HW", "HM"], ["HS"], bias=-1407.0)
-        half = 2 * C
-        cp(B("FT", 0, half), B(X).indirect(B("L2", 0, 44)), xk + dk + ["L2"], ["FTa"])
-        act(B("FT", half, 4 * C), B(X).indirect(B("L2", 44, 88)), AF.Copy, xk + dk + ["L2"], ["FTb"])
-        quant("FQ", "FS", "FT", C, ["FTa", "FTb"])
-        for b in (2, 3):
-            act(B("F64", b, 4 * C, 4), B("FT", b, 4 * C, 4), AF.Copy, ["FTa", "FTb"], ["F64%d" % b], scale=64.0)
-        for b in (0, 1):
-            ts(B("F64", b, 4 * C, 4), B("FT", b, 4 * C, 4), 64.0, None, A.mult, None, ["FTa", "FTb"], ["F64%d" % b])
+        cp(B("FT", 0, 4 * H), B(X).indirect(B("L2", 0, 44)), xk + dk + ["L2"], ["FT0"])
+        act(B("FT", 4 * H, 4 * C), B(X).indirect(B("L2", 44, 88)), AF.Copy, xk + dk + ["L2"], ["FT1"])
+        act(B("F64", 4 * H, 4 * C), B("FT", 4 * H, 4 * C), AF.Copy, ["FT1"], ["F641"], scale=64.0)
+        quant("FQ", "FS", "FT", H, ["FT0"], 0, "FQ0")
+        ts(B("F64", 0, 4 * H), B("FT", 0, 4 * H), 64.0, None, A.mult, None, ["FT0"], ["F640"])
+        quant("FQ", "FS", "FT", H, ["FT1"], H, "FQ1")
         Y = "TD%d" % (t + 1)
-        for b in range(4):
-            mm("RB%d" % b, C, B("WQ", 128 * b, 128 * b + 128), B("WP", 128 * b, 128 * b + 128), B("FQ"), B("FS"), True, True, ["WQ", "WP", "FQ"])
-            tt(B("AC%d" % b), B("RB%d" % b, 0, C), B("F64", b, 4 * C, 4), A.add, ["RB%d" % b, "F64%d" % b], ["AC%d" % b])
-            act(B(Y, b, 4 * C, 4), B("AC%d" % b), AF.Copy, ["AC%d" % b], [Y + "x%d" % b], scale=0.015625)
+        for h in range(2):
+            for b in range(4):
+                bank, ac = HALF[h][b], "AC%d%d" % (h, b)
+                mm(bank, H, B("WQ", 128 * b, 128 * b + 128), B("WP", 128 * b, 128 * b + 128), B("FQ", H * h, H * h + H), B("FS", H * h, H * h + H),
+                   True, True, ["WQ", "WP", "FQ%d" % h])
+                tt(B("AC%d" % b, H * h, H * h + H), B(bank, 0, H), B("F64", 4 * H * h + b, 4 * H * (h + 1), 4), A.add, [bank, "F64%d" % h], [ac])
+                act(B(Y, 4 * H * h + b, 4 * H * (h + 1), 4), B("AC%d" % b, H * h, H * h + H), AF.Copy, [ac], [Y + "x%d%d" % (h, b)], scale=0.015625)
+        pack(t + 1)
 
-    quant("TQ3", "TS3", "TD3", C, ["TD3x%d" % b for b in range(4)])
-    mm("PB", C, B("VQ"), B("VS"), B("TQ3"), B("TS3"), True, True, ["VQ", "TQ3"])
-    act(B("HT"), B("HS"), AF.Copy, ["HS"], ["HT"], scale=-176.0)
     stores = []
 
     def store(q, out, in_, rd):
         before(q, rd, [])
-        stores.append("od" if q == "y" else "ot1")
+        stores.append("od" if q == "y" else "os")
         eng[q].dma_start(out, in_).then_inc(T.sem[stores[-1]], 16)
 
-    store("y", T.oc[:, :], B("TQ3").bitcast(dt.uint8), ["TQ3"])
-    for k in range(4):
-        store("y", T.osc[4 * k:4 * k + 4, :], T.TS3[32 * k:32 * k + 4, :], ["TQ3"])
-    act(B("YB"), B("PB", 0, C), AF.Copy, ["PB"], ["YB"])
+    for h in range(2):
+        mm("RB%d" % h, H, B("VQ"), B("VS"), B("TQ3", H * h, H * h + H), B("TS3", H * h, H * h + H), True, True, ["VQ", "TQ3h%d" % h])
+        store("y", T.oc[:, 4 * H * h:4 * H * (h + 1)], B("TQ3", H * h, H * h + H).bitcast(dt.uint8), ["TQ3h%d" % h])
+    cp(B("YB", 0, H), B("RB0", 0, H), ["RB0"], ["YB0"])
+    act(B("HT"), B("HS"), AF.Copy, ["HS"], ["HT"], scale=-176.0)
+    act(B("YB", H, C), B("RB1", 0, H), AF.Copy, ["RB1"], ["YB1"])
     tt(B("HO"), B("HQ"), B("HT"), A.add, ["HQ", "HT"], ["HO"])
-    store("y", T.y[:, :], B("YB"), ["YB"])
+    for k in range(4):
+        store("y", T.osc[4 * k:4 * k + 4, :], T.TS3[32 * k:32 * k + 4, :], ["TQ3h0", "TQ3h1"])
+    store("s", T.y[:, H:C], B("YB", H, C), ["YB1"])
+    store("y", T.y[:, 0:H], B("YB", 0, H), ["YB0"])
     store("s", T.ot[:, :], T.HO[0:128:16, :], ["HO"])
     g.wait_ge(T.sem.sent, sent[0])
     for q in ("v", "s", "p", "g"):
         g.wait_ge(T.sem["c" + q], count[q])
     g.wait_ge(T.sem.od, 16 * stores.count("od"))
-    g.wait_ge(T.sem.ot1, 16 * stores.count("ot1"))
+    g.wait_ge(T.sem["os"], 16 * stores.count("os"))

@@ -1,10 +1,12 @@
 from concourse.mybir import dt, AluOpType, ActivationFunctionType
 
 C = 352
-H = C // 2
 ROUNDS = 3
+PIECES = [(0, 128), (128, C)]
 SLOTS = [(352, [0, 21, 20, 19]), (288, [18, 17, 16, 15]), (224, [14, 13, 12, 11]), (160, [10, 9, 8, 7]),
          (128, [6, 5, 4, 3]), (128, [2, 1])]
+ON_S = [21, 16]
+QAT = 1
 
 SCRATCH = {}
 
@@ -15,14 +17,13 @@ def _add(where, dtype, **names):
 
 
 F8 = "float8_e4m3fn_x4"
-_add("sbuf", "bfloat16", UB=512, VB=512, TD0=8 * C, TD1=8 * C, TD2=8 * C, TD3=4 * C, FT=4 * C, F64=4 * C,
-     EBA=2048, W1B=512, JUNK=8 * 22 * 21)
+_add("sbuf", "bfloat16", UB=512, VB=512, TD0=8 * C, TD1=8 * C, TD2=8 * C, TD3=4 * C, FT=4 * C, FF=4 * C,
+     ZO=516, ZE0=516, ZE1=516, BD=512, W1B=512, JUNK=8 * 22 * 21)
 _add("sbuf", F8, UQ=128, UU=256, VQ=128, WQ=512, FQ=C, EQA=512, W1Q=128, GQA=1280)
 _add("sbuf", "uint8", US=128, UV=256, VS=128, WP=512, FS=C, ESA=512, W1S=128, GSA=1280)
 PART = {}
 for _i in range(4):
-    PART["EB%d" % _i], PART["EQ%d" % _i], PART["ES%d" % _i] = ("EBA", 512 * _i, 512), ("EQA", 128 * _i, 128), ("ESA", 128 * _i, 128)
-    PART["AC%d" % _i], PART["ET%d" % _i] = ("ACA", C * _i, C), ("ETA", 512 * _i, 512)
+    PART["EQ%d" % _i], PART["ES%d" % _i] = ("EQA", 128 * _i, 128), ("ESA", 128 * _i, 128)
 for _t in range(ROUNDS + 1):
     _add("sbuf", F8, **{"TQ%d" % _t: C})
     _add("sbuf", "uint8", **{"TS%d" % _t: C})
@@ -36,13 +37,13 @@ for _m, (_w, _k) in enumerate(SLOTS):
         PART["%s%d" % (_n, _m)] = (_n + "A", sum(w for w, k in SLOTS[:_m]), _w)
 _add("sbuf", "uint16", OFU=16, DST=22, L2=88)
 _add("sbuf", "int32", IU=16, PI=2, KI=4)
-_add("sbuf", "float32", C16=C, C4=C, M512=512, BD=512, CWI=22, NPB=4, N4=C, NV=C, Q5=C, KF=4, COL=8,
-     NE16=C, NE4=C, MK=C, D0=C, RST=C, PKA=C, PKB=C, CW=22, ETA=2048,
+_add("sbuf", "float32", C16=C, C4=C, PL=C, DR=C, CWI=22, N4=C, NV=C, Q5=C, KF=4, COL=8,
+     NE16=C, NE4=C, D4=C, MK=C, D0=C, RST=C, PKA=C, PKB=C, CW=22,
      DM=C, PX=C, DS=C, RS=22, TA=22, TB=22, PKX=C, RF=22, SGN=C, SGP=C, NC=2, WC1=2, BC=2, SC=2,
-     SQ=C, SG2=C, SEG=C, NSEG=C, RKR=C, NKR=C, KP=C, E1=C, GX=C, GP=C, MM=22, DD=22,
-     HW=992, HP=C, ACA=4 * C, YB=C, HQ=C, HS=C, HT=C, HO=C)
+     SQ=C, SG2=C, RKR=C, NKR=C, KP=C, E1=C, GX=C, GP=C, MM=22, DD=22,
+     HW=992, HP=C, YB=C, HQ=C, HS=C, HT=C, HO=C)
 PSUM = ["PB", "NB", "CS", "RB0", "RB1", "RB2", "RB3", "RB4"]
-HALF = [["RB0", "RB1", "RB2", "RB3"], ["RB4", "NB", "CS", "PB"]]
+BANKS = [["RB0", "RB1", "RB2", "RB3"], ["RB4", "NB", "CS", "PB"]]
 for _n in PSUM:
     SCRATCH[_n] = ("psum", [128, 512], "float32")
 
@@ -136,8 +137,8 @@ def rank_program(g, core, T, topo):
         return ["TD%dx%d%d" % (t, h, b) for b in range(4)]
 
     dma("s", B("UB"), T.u[:, :], "lu", 16, [], ["UB"])
-    dma("y", B("TD0", 0, 4 * H), T.x[:, 0:4 * H], "lx0", 16, [], xkeys(0, 0))
-    dma("y", B("TD0", 4 * H, 4 * C), T.x[:, 4 * H:4 * C], "lx1", 16, [], xkeys(0, 1))
+    for h, (a, z) in enumerate(PIECES):
+        dma("y", B("TD0", 4 * a, 4 * z), T.x[:, 4 * a:4 * z], "lx%d" % h, 16, [], xkeys(0, h))
 
     def iota(name, pattern, base, cm, flag=True):
         n = 1
@@ -150,11 +151,17 @@ def rank_program(g, core, T, topo):
 
     iota("IU", [[1, 2], [16, 8]], 0, 0, False)
     iota("PI", [[0, 2]], 0, 1, False)
-    iota("NPB", [[-1, 4]], 0, -4)
-    iota("CWI", [[-16, 22]], 351, 0)
     iota("C16", [[0, 22], [1, 16]], 0, 0)
-    iota("M512", [[1, 512]], 0, 0)
     iota("BD", [[1, 8], [0, 64]], 0, 0)
+    iota("CWI", [[-16, 22]], 351 - 16 * len(ON_S), 0)
+    op("v", lambda: V.memset(B("ZO"), 1.0), [], ["ZO"])
+    for m, (w, ks) in enumerate(SLOTS):
+        lo = 4 * (0 if len(ks) < 4 else 16 * ks[-1])
+        keys = ["G%d.%d" % (m, b) for b in range(4)]
+        if m > 3:
+            act(B("G%d" % m, lo, 4 * w), B("ZO", lo, 4 * w), AF.Copy, ["ZO"], keys, scale=0.0)
+        else:
+            op("v", (lambda m=m, w=w, lo=lo: V.memset(B("G%d" % m, lo, 4 * w), 0.0)), [], keys)
     cp(B("OFU"), B("IU"), ["IU"], ["OFU"])
     ts(B("KI", 0, 1), B("PI", 0, 1), 15, None, A.bitwise_and, None, ["PI"], ["KI0"])
     ts(B("KI", 1, 2), B("PI", 0, 1), 4, None, A.arith_shift_right, None, ["PI"], ["KI1"])
@@ -162,27 +169,20 @@ def rank_program(g, core, T, topo):
     ts(B("KI", 3, 4), B("PI", 0, 1), 3, None, A.bitwise_and, None, ["PI"], ["KI3"])
     cp(B("KF"), B("KI"), ["KI0", "KI1", "KI2", "KI3"], ["KF"])
     ci, cg, cq, cr = [B("KF", j, j + 1) for j in range(4)]
-    ts(B("NE16"), B("C16"), ci, None, A.not_equal, None, ["C16", "KF"], ["NE16"])
+    ts(B("MK"), B("C16"), ci, -1e29, A.not_equal, A.mult, ["C16", "KF"], ["MK"])
+    act(B("D0"), B("C16"), AF.Copy, ["C16"], ["D0"], bias=-0.5e29, scale=1e29)
+    act(B("RST"), B("C16"), AF.Sign, ["C16"], ["RST"])
+    act(B("NE16"), B("MK"), AF.Sign, ["MK"], ["NE16"], scale=-1.0)
+    act(B("PKA"), B("NE16"), AF.Copy, ["NE16"], ["PKA"], bias=-262144.0, scale=262144.0 + 1024.0)
+    for j in range(2):
+        op("g", (lambda j=j: g.affine_select(B("ZE%d" % j), B("ZO"), [[1, 516]], A.is_equal, 0.0, -2 - j, -4)), ["ZO"], ["ZE%d" % j])
     for j, (m, a) in enumerate([(-1024.0, 15360.0 + 224.0), (1024.0, -15361.0), (-1025.0, 15360.0), (4096.0, -12288.0)]):
         ts(B("COL", j, j + 1), cq if j == 3 else ci, m, a, A.mult, A.add, ["KF"], ["COL%d" % j])
-    op("v", lambda: V.memset(B("RS", 0, 2), 0.0), [], ["RS0", "RS1"])
-    tt(B("COL", 4, 5), B("COL", 3, 4), cr, A.add, ["COL3", "KF"], ["COL4"])
-    ts(B("CW"), B("CWI"), B("COL", 2, 3), None, A.add, None, ["CWI", "COL2"], ["CW"])
-    for m, (w, ks) in enumerate(SLOTS):
-        lo = 0 if len(ks) < 4 else 16 * ks[-1]
-        op("v", (lambda m=m, w=w, lo=lo: V.memset(B("G%d" % m, 4 * lo, 4 * w), 0.0)), [], ["G%d.%d" % (m, b) for b in range(4)])
-    act(B("D0"), B("C16"), AF.Copy, ["C16"], ["D0"], bias=-0.5e29, scale=1e29)
-    act(B("MK"), B("NE16"), AF.Copy, ["NE16"], ["MK"], scale=-1e29)
-    act(B("PKA"), B("NE16"), AF.Copy, ["NE16"], ["PKA"], bias=-262144.0, scale=262144.0 + 1024.0)
+    ts(B("W1B"), B("BD"), cg, None, A.is_equal, None, ["BD", "KF"], ["W1B"])
+    quant("W1Q", "W1S", "W1B", 128, ["W1B"])
     quant("UQ", "US", "UB", 128, ["UB"])
     op("v", lambda: V.tensor_copy(B("UU").bitcast(dt.uint32), B("UQ").bitcast(dt.uint32).indirect(B("OFU"))), ["UQ", "OFU"], ["UU"])
-    for b in range(4):
-        act(B("ET%d" % b), B("M512"), AF.Abs, ["M512", "NPB"], ["ET%d" % b], bias=B("NPB", b, b + 1))
     act(B("UV"), B("US").indirect(B("OFU")), AF.Copy, ["UQ", "OFU"], ["UV"])
-    for b in range(4):
-        act(B("EB%d" % b), B("ET%d" % b), AF.Relu, ["ET%d" % b], ["EB%d" % b], bias=1.0, scale=-1.0)
-    act(B("RST"), B("C16"), AF.Sign, ["C16"], ["RST"])
-    ts(B("W1B"), B("BD"), cg, None, A.is_equal, None, ["BD", "KF"], ["W1B"])
     dma("y", B("WQ").bitcast(dt.uint8), T.wc[:, :], "lwc", 16, ["UQ"], ["WQ"])
     dma("y", B("WP"), T.ws[:, :], "lws", 16, [], ["WP"])
     dma("y", B("VB"), T.v[:, :], "lv", 16, [], ["VB"])
@@ -200,36 +200,41 @@ def rank_program(g, core, T, topo):
         for k in wr:
             wrote[k] = ("r", (sem, val, {}))
 
-    def pack(t):
-        for h in range(2):
-            quant("TQ%d" % t, "TS%d" % t, "TD%d" % t, H, xkeys(t, h), H * h, "TQ%dh%d" % (t, h))
+    def pack(t, h):
+        a, z = PIECES[h]
+        quant("TQ%d" % t, "TS%d" % t, "TD%d" % t, z - a, xkeys(t, h), a, "TQ%dh%d" % (t, h))
 
-    pack(0)
-    quant("W1Q", "W1S", "W1B", 128, ["W1B"])
+    pack(0, 0)
+    pack(0, 1)
+    (_, m0), (m1, _) = PIECES
     for t in range(ROUNDS):
         X, tq, tsc, lo, lr, rq, rp = ["%s%d" % (n, t) for n in ("TD", "TQ", "TS", "LO", "LR", "RQ", "RP")]
         tk = [tq + "h0", tq + "h1"]
         xk = xkeys(t, 0) + xkeys(t, 1)
         dk = [X + "d%d" % b for b in range(4)]
+        last = t == ROUNDS - 1
         send(t, B(rq).bitcast(dt.uint8), B(tq).bitcast(dt.uint8), "ad%d" % t, 2 * ne[t], tk, [rq])
         send(t, B(rp), B(tsc), "ad%d" % t, 2 * ne[t], tk, [rp])
-        mm("RB0", H, B("UU", 0, 128), B("UV", 0, 128), B(tq, 0, H), B(tsc, 0, H), True, True, ["UU", "UV", tk[0]])
+        mm("RB0", m0, B("UU", 0, 128), B("UV", 0, 128), B(tq, 0, m0), B(tsc, 0, m0), True, True, ["UU", "UV", tk[0]])
         mm("PB", C, B("UU", 0, 128), B("UV", 0, 128), B(tq), B(tsc), True, True, ["UU", "UV"] + tk)
+        mm("RB1", C, B("UU", 0, 128), B("UV", 0, 128), B(tq), B(tsc), True, True, ["UU", "UV"] + tk)
         mm("NB", C, B("UU", 128, 256), B("UV", 128, 256), B(tq), B(tsc), True, True, ["UU", "UV"] + tk)
         if t == 0:
+            iota("PL", [[1, C]], 0, 0)
             iota("N4", [[4, C]], 0, 0)
             iota("Q5", [[1, C]], 512, 0)
             iota("C4", [[0, 88], [1, 4]], 0, 0)
             iota("NV", [[4, C]], 4 * C, 0)
-        act(B("SGN"), B("NB", 0, C), AF.Sign, ["NB"], ["SGN"])
-        act(B("SGP"), B("SGN"), AF.Relu, ["SGN"], ["SGP", "NC"], accum_out=B("NC", 0, 1))
-        act(B("WC1", 0, 1), B("NC", 0, 1), AF.Relu, ["NC"], ["WC1"], bias=224.0, scale=-1.0)
-        act(B("BC", 0, 1), B("WC1", 0, 1), AF.Copy, ["WC1"], ["BC"], bias=-287.5)
-        act(B("SC", 0, 1), B("WC1", 0, 1), AF.Identity, ["WC1", "COL0"], ["SC"], bias=B("COL", 0, 1), scale=-1.0)
         for h, bank in enumerate(("RB0", "PB")):
-            a, z = H * h, H * h + H
+            a, z = PIECES[h]
             tt(B("DM", a, z), B(bank, a, z), B("MK", a, z), A.add, [bank, "MK"], ["DM%d" % h])
             scan(B("PX", a, z), B("D0", a, z), B("DM", a, z), -1e29, A.min, A.max, ["D0", "DM%d" % h], ["PX%d" % h])
+        for k in ON_S:
+            n = 16 * k
+            act(B("DR", 0, n), B("RB1", 0, n), AF.Relu, ["RB1", "PX0", "PX1"], ["DR"], bias=B("PX", n + 15, n + 16), scale=-1.0)
+            m, b = [(m, ks.index(k)) for m, (w, ks) in enumerate(SLOTS) if k in ks][0]
+            act(B("G%d" % m, b, 4 * n, 4), B("DR", 0, n), AF.Sign, ["DR"], ["G%d.%d" % (m, b), "RS%d" % k], scale=-1.0,
+                accum_out=B("RS", k, k + 1))
         queue = []
 
         def flush(m):
@@ -242,40 +247,54 @@ def rank_program(g, core, T, topo):
                 gk = "G%d.%d" % (m, b)
                 if k == 0:
                     tt(B("G0", 0, 4 * C, 4), B("PB", 0, C), B("PX"), A.is_gt, ["PB", "PX0", "PX1"], [gk])
-                else:
+                elif k not in ON_S:
                     n = 16 * k
                     ts(B("G%d" % m, b, 4 * n, 4), B("PB", 0, n), B("PX", n + 15, n + 16), None, A.is_ge, None, ["PB", "PX0", "PX1"], [gk])
                     act(B("JUNK", 8 * k * (k - 1), 8 * k * (k + 1)), B("G%d" % m, b, 4 * n, 4), AF.Copy, [gk], ["J%d" % k, "RS%d" % k],
                         accum_out=B("RS", k, k + 1))
                 if b == 0 and queue:
                     flush(queue.pop())
-                if m == 0 and b == 2:
-                    scan(B("DS"), B("RST"), B("G0", 0, 4 * C, 4), 0.0, A.mult, A.add, ["RST", "G0.0"], ["DS"])
             queue.append(m)
+        if t == 0:
+            op("v", lambda: V.memset(B("RS", 0, 1), 0.0), [], ["RS0"])
         flush(queue.pop())
+        scan(B("DS"), B("RST"), B("G0", 0, 4 * C, 4), 0.0, A.mult, A.add, ["RST", "G0.0"], ["DS"])
+        if t == 0:
+            ts(B("CW"), B("CWI"), B("COL", 2, 3), None, A.add, None, ["CWI", "COL2"], ["CW"])
+            for k in ON_S:
+                ts(B("CW", k, k + 1), B("CW", k, k + 1), float(16 * k), None, A.add, None, ["CW"], ["CW"])
+            for k in sorted(ON_S):
+                ts(B("CW", k, 22), B("CW", k, 22), 16.0, None, A.add, None, ["CW"], ["CW"])
+            tt(B("COL", 4, 5), B("COL", 3, 4), cr, A.add, ["COL3", "KF"], ["COL4"])
+        act(B("SGN"), B("NB", 0, C), AF.Sign, ["NB"], ["SGN"])
+        act(B("SGP"), B("SGN"), AF.Relu, ["SGN"], ["SGP", "NC"], accum_out=B("NC", 0, 1))
+        act(B("WC1", 0, 1), B("NC", 0, 1), AF.Relu, ["NC"], ["WC1"], bias=224.0, scale=-1.0)
+        act(B("BC", 0, 1), B("WC1", 0, 1), AF.Copy, ["WC1"], ["BC"], bias=-287.5)
+        act(B("SC", 0, 1), B("WC1", 0, 1), AF.Identity, ["WC1", "COL0"], ["SC"], bias=B("COL", 0, 1), scale=-1.0)
+        act(B("SQ"), B("PL"), AF.Square, ["PL", "BC"], ["SQ"], bias=B("BC", 0, 1))
+        act(B("SG2"), B("SQ"), AF.Sign, ["SQ"], ["SG2"], bias=4096.0, scale=-1.0)
         tt(B("TA"), B("CW"), B("DS", 15, C, 16), A.add, ["CW", "DS"], ["TA"])
         tt(B("TB"), B("TA"), B("RS"), A.add, ["TA"] + ["RS%d" % k for k in range(22)], ["TB"])
         scan(B("PKX"), B("PKA"), B("CS", 0, C), 0.0, A.add, A.max, ["PKA", "CS"], ["PKX"])
         tt(B("RF"), B("TB"), B("PKX", 15, C, 16), A.subtract, ["TB", "PKX"], ["RF"])
         cp(B(lo), B("RF"), ["RF"], [lo])
         send(t, B(lr), B(lo), "al%d" % t, ne[t], [lo], [lr])
-        act(B("SQ"), B("M512", 0, C), AF.Square, ["M512", "BC"], ["SQ"], bias=B("BC", 0, 1))
-        act(B("SG2"), B("SQ"), AF.Sign, ["SQ"], ["SG2"], bias=4096.0, scale=-1.0)
-        act(B("NSEG"), B("SG2"), AF.Relu, ["SG2"], ["NSEG"], scale=-1.0)
-        act(B("SEG"), B("SG2"), AF.Relu, ["SG2"], ["SEG"])
-        act(B("NKR"), B("NSEG").indirect(B(lo)), AF.Copy, ["NSEG", lo], ["NKR"])
+        act(B("NKR"), B("SG2").indirect(B(lo)), AF.Relu, ["SG2", lo], ["NKR"], scale=-1.0)
         op("v", lambda: V.tensor_copy(B("HW").indirect(B(lo)), B("N4")), ["N4", lo], ["HW"])
-        tt(B("RKR"), B("SEG").indirect(B(lo)), B("Q5"), A.mult, ["SEG", lo, "Q5"], ["RKR"])
+        tt(B("RKR"), B("SG2").indirect(B(lo)), B("Q5"), A.mult, ["SG2", lo, "Q5"], ["RKR"])
         if t == 0:
             for b in range(4):
-                quant("EQ%d" % b, "ES%d" % b, "EB%d" % b, 128, ["EB%d" % b])
-            ts(B("NE4"), B("C4"), cq, None, A.not_equal, None, ["C4", "KF"], ["NE4"])
+                ze, at = "ZE%d" % (b % 2), 2 + b % 2 - b
+                op("v", (lambda b=b, ze=ze, at=at: V.quantize_mx(B("EQ%d" % b), B("ES%d" % b), B(ze, at, at + 512))), [ze], ["EQ%d" % b])
+        if t == 1:
             quant("VQ", "VS", "VB", 128, ["VB"])
         for b in range(4):
             mm("RB%d" % b, C, B("EQ%d" % b), B("ES%d" % b), B(rq), B(rp), True, True, ["EQ%d" % b, rq, rp])
         for b in range(4):
             act(B(X, 4 * C + b, 8 * C, 4), B("RB%d" % b, 0, C), AF.Copy, ["RB%d" % b], [dk[b]])
         if t == 0:
+            act(B("D4"), B("C4"), AF.Abs, ["C4", "KF"], ["D4"], bias=cq, scale=-1.0)
+            act(B("NE4"), B("D4"), AF.Sign, ["D4"], ["NE4"])
             act(B("PKB"), B("NE4"), AF.Copy, ["NE4"], ["PKB"], bias=-262144.0, scale=262144.0 + 4096.0)
         op("v", lambda: V.tensor_copy(B("KP").indirect(B(lr)), B("NKR")), ["NKR", lr], ["KP"])
         scan(B("E1"), B("KP"), B("KP"), 0.0, A.add, A.max, ["KP"], ["E1"])
@@ -288,24 +307,26 @@ def rank_program(g, core, T, topo):
         op("v", lambda: V.tensor_copy(B("HW").indirect(B("DST")), B("NV")), ["NV", "DST"], ["HW"])
         scan(B("HP"), B("PKB"), B("HW", 0, C), 0.0, A.add, A.max, ["PKB", "HW"], ["HP"])
         ts(B("L2"), B("HP", 3, C, 4), B("COL", 4, 5), None, A.add, None, ["HP", "COL4"], ["L2"])
-        if t == ROUNDS - 1:
+        if last:
+            act(B("HS"), B("HW", 0, C), AF.Sign, ["HW"], ["HS"], bias=-1407.0)
+        ts(B("FT", 0, 4 * m0), B(X).indirect(B("L2", 0, m0 // 4)), 0.015625, None, A.mult, None, xk + dk + ["L2"], ["FT0"])
+        act(B("FT", 4 * m1, 4 * C), B(X).indirect(B("L2", m1 // 4, 88)), AF.Copy, xk + dk + ["L2"], ["FT1"], scale=0.015625)
+        quant("FQ", "FS", "FT", m0, ["FT0"], 0, "FQ0")
+        ts(B("FF", 0, 4 * m0), B("FT", 0, 4 * m0), 64.0, None, A.mult, None, ["FT0"], ["FF0"])
+        act(B("FF", 4 * m1, 4 * C), B("FT", 4 * m1, 4 * C), AF.Copy, ["FT1"], ["FF1"], scale=64.0)
+        if last:
             act(B("HQ"), B("HW", 0, C), AF.Copy, ["HW"], ["HQ"], bias=-176.0, scale=0.25)
-            act(B("HS"), B("HW", 0, C), AF.Sign, ["HW", "HM"], ["HS"], bias=-1407.0)
-        cp(B("FT", 0, 4 * H), B(X).indirect(B("L2", 0, 44)), xk + dk + ["L2"], ["FT0"])
-        act(B("FT", 4 * H, 4 * C), B(X).indirect(B("L2", 44, 88)), AF.Copy, xk + dk + ["L2"], ["FT1"])
-        act(B("F64", 4 * H, 4 * C), B("FT", 4 * H, 4 * C), AF.Copy, ["FT1"], ["F641"], scale=64.0)
-        quant("FQ", "FS", "FT", H, ["FT0"], 0, "FQ0")
-        ts(B("F64", 0, 4 * H), B("FT", 0, 4 * H), 64.0, None, A.mult, None, ["FT0"], ["F640"])
-        quant("FQ", "FS", "FT", H, ["FT1"], H, "FQ1")
+            act(B("HT"), B("HS"), AF.Copy, ["HS"], ["HT"], scale=-176.0)
         Y = "TD%d" % (t + 1)
-        for h in range(2):
+        for h, (a, z) in enumerate(PIECES):
             for b in range(4):
-                bank, ac = HALF[h][b], "AC%d%d" % (h, b)
-                mm(bank, H, B("WQ", 128 * b, 128 * b + 128), B("WP", 128 * b, 128 * b + 128), B("FQ", H * h, H * h + H), B("FS", H * h, H * h + H),
+                bank = BANKS[h][b]
+                mm(bank, z - a, B("WQ", 128 * b, 128 * b + 128), B("WP", 128 * b, 128 * b + 128), B("FQ", a, z), B("FS", a, z),
                    True, True, ["WQ", "WP", "FQ%d" % h])
-                tt(B("AC%d" % b, H * h, H * h + H), B(bank, 0, H), B("F64", 4 * H * h + b, 4 * H * (h + 1), 4), A.add, [bank, "F64%d" % h], [ac])
-                act(B(Y, 4 * H * h + b, 4 * H * (h + 1), 4), B("AC%d" % b, H * h, H * h + H), AF.Copy, [ac], [Y + "x%d%d" % (h, b)], scale=0.015625)
-        pack(t + 1)
+                tt(B(Y, 4 * a + b, 4 * z, 4), B(bank, 0, z - a), B("FF", 4 * a + b, 4 * z, 4), A.add, [bank, "FF%d" % h], [Y + "x%d%d" % (h, b)])
+                if (h, b) == (0, QAT):
+                    quant("FQ", "FS", "FT", C - m1, ["FT1"], m1, "FQ1")
+            pack(t + 1, h)
 
     stores = []
 
@@ -314,17 +335,14 @@ def rank_program(g, core, T, topo):
         stores.append("od" if q == "y" else "os")
         eng[q].dma_start(out, in_).then_inc(T.sem[stores[-1]], 16)
 
-    for h in range(2):
-        mm("RB%d" % h, H, B("VQ"), B("VS"), B("TQ3", H * h, H * h + H), B("TS3", H * h, H * h + H), True, True, ["VQ", "TQ3h%d" % h])
-        store("y", T.oc[:, 4 * H * h:4 * H * (h + 1)], B("TQ3", H * h, H * h + H).bitcast(dt.uint8), ["TQ3h%d" % h])
-    cp(B("YB", 0, H), B("RB0", 0, H), ["RB0"], ["YB0"])
-    act(B("HT"), B("HS"), AF.Copy, ["HS"], ["HT"], scale=-176.0)
-    act(B("YB", H, C), B("RB1", 0, H), AF.Copy, ["RB1"], ["YB1"])
+    for h, (a, z) in enumerate(PIECES):
+        mm("RB%d" % h, z - a, B("VQ"), B("VS"), B("TQ3", a, z), B("TS3", a, z), True, True, ["VQ", "TQ3h%d" % h])
+        store("y", T.oc[:, 4 * a:4 * z], B("TQ3", a, z).bitcast(dt.uint8), ["TQ3h%d" % h])
+        act(B("YB", a, z), B("RB%d" % h, 0, z - a), AF.Copy, ["RB%d" % h], ["YB%d" % h])
+        store("s", T.y[:, a:z], B("YB", a, z), ["YB%d" % h])
     tt(B("HO"), B("HQ"), B("HT"), A.add, ["HQ", "HT"], ["HO"])
     for k in range(4):
         store("y", T.osc[4 * k:4 * k + 4, :], T.TS3[32 * k:32 * k + 4, :], ["TQ3h0", "TQ3h1"])
-    store("s", T.y[:, H:C], B("YB", H, C), ["YB1"])
-    store("y", T.y[:, 0:H], B("YB", 0, H), ["YB0"])
     store("s", T.ot[:, :], T.HO[0:128:16, :], ["HO"])
     g.wait_ge(T.sem.sent, sent[0])
     for q in ("v", "s", "p", "g"):

from concourse.mybir import dt, AluOpType, ActivationFunctionType

C = 352
ROUNDS = 3
PIECES = [(0, 128), (128, C)]
SLOTS = [(352, [0, 21, 20, 19]), (288, [18, 17, 16, 15]), (224, [14, 13, 12, 11]), (160, [10, 9, 8, 7]),
         (128, [6, 5, 4, 3]), (128, [2, 1])]
ON_S = [21, 16]
QAT = 1

SCRATCH = {}


def _add(where, dtype, **names):
    for n, w in names.items():
        SCRATCH[n] = (where, [128, w], dtype)


F8 = "float8_e4m3fn_x4"
_add("sbuf", "bfloat16", UB=512, VB=512, TD0=8 * C, TD1=8 * C, TD2=8 * C, TD3=4 * C, FT=4 * C, FF=4 * C,
     ZO=516, ZE0=516, ZE1=516, BD=512, W1B=512, JUNK=8 * 22 * 21)
_add("sbuf", F8, UQ=128, UU=256, VQ=128, WQ=512, FQ=C, EQA=512, W1Q=128, GQA=1280)
_add("sbuf", "uint8", US=128, UV=256, VS=128, WP=512, FS=C, ESA=512, W1S=128, GSA=1280)
PART = {}
for _i in range(4):
    PART["EQ%d" % _i], PART["ES%d" % _i] = ("EQA", 128 * _i, 128), ("ESA", 128 * _i, 128)
for _t in range(ROUNDS + 1):
    _add("sbuf", F8, **{"TQ%d" % _t: C})
    _add("sbuf", "uint8", **{"TS%d" % _t: C})
for _t in range(ROUNDS):
    _add("sbuf", F8, **{"RQ%d" % _t: C})
    _add("sbuf", "uint8", **{"RP%d" % _t: C})
    _add("sbuf", "uint16", **{"LO%d" % _t: 22, "LR%d" % _t: 22})
for _m, (_w, _k) in enumerate(SLOTS):
    _add("sbuf", "bfloat16", **{"G%d" % _m: 4 * _w})
    for _n in ("GQ", "GS"):
        PART["%s%d" % (_n, _m)] = (_n + "A", sum(w for w, k in SLOTS[:_m]), _w)
_add("sbuf", "uint16", OFU=16, DST=22, L2=88)
_add("sbuf", "int32", IU=16, PI=2, KI=4)
_add("sbuf", "float32", C16=C, C4=C, PL=C, DR=C, CWI=22, N4=C, NV=C, Q5=C, KF=4, COL=8,
     NE16=C, NE4=C, D4=C, MK=C, D0=C, RST=C, PKA=C, PKB=C, CW=22,
     DM=C, PX=C, DS=C, RS=22, TA=22, TB=22, PKX=C, RF=22, SGN=C, SGP=C, NC=2, WC1=2, BC=2, SC=2,
     SQ=C, SG2=C, RKR=C, NKR=C, KP=C, E1=C, GX=C, GP=C, MM=22, DD=22,
     HW=992, HP=C, YB=C, HQ=C, HS=C, HT=C, HO=C)
PSUM = ["PB", "NB", "CS", "RB0", "RB1", "RB2", "RB3", "RB4"]
BANKS = [["RB0", "RB1", "RB2", "RB3"], ["RB4", "NB", "CS", "PB"]]
for _n in PSUM:
    SCRATCH[_n] = ("psum", [128, 512], "float32")

SEMAPHORES = ["cv", "cs", "cp", "cg", "lx0", "lx1", "lu", "lv", "lwc", "lws", "sent", "od", "os"] + \
    ["ad%d" % t for t in range(ROUNDS)] + ["al%d" % t for t in range(ROUNDS)]


def rank_program(g, core, T, topo):
    rank = T.rank_of(core)
    if rank is None:
        return
    A, AF = AluOpType, ActivationFunctionType
    eng = {"v": g.vector, "s": g.scalar, "p": g.tensor, "g": g, "y": g.sync}
    count = {"v": 0, "s": 0, "p": 0, "g": 0}
    seen = {q: {} for q in eng}
    wrote, reads_of = {}, {}

    def need(q, toks):
        toks = sorted(toks, key=lambda k: -sum(k[2].values()))
        for sem, val, past in toks:
            if seen[q].get(sem, 0) >= val:
                continue
            eng[q].wait_ge(T.sem[sem], val)
            seen[q][sem] = val
            for s, v in past.items():
                seen[q][s] = max(seen[q].get(s, 0), v)

    def before(q, rd, wr):
        toks = []
        for k in rd:
            if k in wrote:
                toks.append(wrote[k][1])
            if k in PSUM:
                toks += [tk for o, tk in reads_of.get(k, {}).items() if o != q]
        for k in wr:
            if k in wrote and not (q == "p" and wrote[k][0] == "p"):
                toks.append(wrote[k][1])
            toks += list(reads_of.get(k, {}).values())
        need(q, toks)

    def after(q, tok, rd, wr):
        for k in rd:
            reads_of.setdefault(k, {})[q] = tok
        for k in wr:
            wrote[k] = (q, tok)
            reads_of[k] = {}

    def op(q, fn, rd, wr):
        before(q, rd, wr)
        count[q] += 1
        tok = ("c" + q, count[q], dict(seen[q]))
        fn().then_inc(T.sem["c" + q], 1)
        after(q, tok, rd, wr)

    def dma(q, out, in_, sem, val, rd, wr):
        before(q, rd, wr)
        eng[q].dma_start(out, in_).then_inc(T.sem[sem], 16)
        after("d" + sem, (sem, val, dict(seen[q])), [], wr)

    def B(name, a=0, b=None, step=1):
        buf, at, n = PART.get(name) or (name, 0, SCRATCH[name][1][1])
        return T[buf][:, at + a:at + (n if b is None else b):step]

    V, S, P = g.vector, g.scalar, g.tensor

    def ts(out, in0, s1, s2, o0, o1, rd, wr):
        if o1 is None:
            op("v", lambda: V.tensor_scalar(out, in0, s1, None, o0), rd, wr)
        else:
            op("v", lambda: V.tensor_scalar(out, in0, s1, s2, o0, o1), rd, wr)

    def tt(out, a, b, o, rd, wr):
        op("v", lambda: V.tensor_tensor(out, a, b, o), rd, wr)

    def cp(out, a, rd, wr):
        op("v", lambda: V.tensor_copy(out, a), rd, wr)

    def scan(out, d0, d1, init, o0, o1, rd, wr):
        op("v", lambda: V.tensor_tensor_scan(out, d0, d1, init, o0, o1), rd, wr)

    def quant(c, s, tile, n, rd, a=0, key=None):
        op("v", lambda: V.quantize_mx(B(c, a, a + n), B(s, a, a + n), B(tile, 4 * a, 4 * (a + n))), rd, [key or c])

    def act(out, in_, f, rd, wr, **kw):
        op("s", lambda: S.activation(out, in_, f, **kw), rd, wr)

    def mm(bank, n, a, asc, b, bsc, first, last, rd):
        op("p", lambda: P.matmul_mx(B(bank, 0, n), a, asc, b, bsc, first, last), rd, [bank])

    def xkeys(t, h):
        return ["TD%dx%d%d" % (t, h, b) for b in range(4)]

    dma("s", B("UB"), T.u[:, :], "lu", 16, [], ["UB"])
    for h, (a, z) in enumerate(PIECES):
        dma("y", B("TD0", 4 * a, 4 * z), T.x[:, 4 * a:4 * z], "lx%d" % h, 16, [], xkeys(0, h))

    def iota(name, pattern, base, cm, flag=True):
        n = 1
        for s, k in pattern:
            n *= k
        if flag:
            op("g", lambda: g.iota(B(name, 0, n), pattern, base, cm, allow_small_or_imprecise_dtypes=True), [], [name])
        else:
            op("g", lambda: g.iota(B(name, 0, n), pattern, base, cm), [], [name])

    iota("IU", [[1, 2], [16, 8]], 0, 0, False)
    iota("PI", [[0, 2]], 0, 1, False)
    iota("C16", [[0, 22], [1, 16]], 0, 0)
    iota("BD", [[1, 8], [0, 64]], 0, 0)
    iota("CWI", [[-16, 22]], 351 - 16 * len(ON_S), 0)
    op("v", lambda: V.memset(B("ZO"), 1.0), [], ["ZO"])
    for m, (w, ks) in enumerate(SLOTS):
        lo = 4 * (0 if len(ks) < 4 else 16 * ks[-1])
        keys = ["G%d.%d" % (m, b) for b in range(4)]
        if m > 3:
            act(B("G%d" % m, lo, 4 * w), B("ZO", lo, 4 * w), AF.Copy, ["ZO"], keys, scale=0.0)
        else:
            op("v", (lambda m=m, w=w, lo=lo: V.memset(B("G%d" % m, lo, 4 * w), 0.0)), [], keys)
    cp(B("OFU"), B("IU"), ["IU"], ["OFU"])
    ts(B("KI", 0, 1), B("PI", 0, 1), 15, None, A.bitwise_and, None, ["PI"], ["KI0"])
    ts(B("KI", 1, 2), B("PI", 0, 1), 4, None, A.arith_shift_right, None, ["PI"], ["KI1"])
    ts(B("KI", 2, 3), B("PI", 0, 1), 15, 2, A.bitwise_and, A.arith_shift_right, ["PI"], ["KI2"])
    ts(B("KI", 3, 4), B("PI", 0, 1), 3, None, A.bitwise_and, None, ["PI"], ["KI3"])
    cp(B("KF"), B("KI"), ["KI0", "KI1", "KI2", "KI3"], ["KF"])
    ci, cg, cq, cr = [B("KF", j, j + 1) for j in range(4)]
    ts(B("MK"), B("C16"), ci, -1e29, A.not_equal, A.mult, ["C16", "KF"], ["MK"])
    act(B("D0"), B("C16"), AF.Copy, ["C16"], ["D0"], bias=-0.5e29, scale=1e29)
    act(B("RST"), B("C16"), AF.Sign, ["C16"], ["RST"])
    act(B("NE16"), B("MK"), AF.Sign, ["MK"], ["NE16"], scale=-1.0)
    act(B("PKA"), B("NE16"), AF.Copy, ["NE16"], ["PKA"], bias=-262144.0, scale=262144.0 + 1024.0)
    for j in range(2):
        op("g", (lambda j=j: g.affine_select(B("ZE%d" % j), B("ZO"), [[1, 516]], A.is_equal, 0.0, -2 - j, -4)), ["ZO"], ["ZE%d" % j])
    for j, (m, a) in enumerate([(-1024.0, 15360.0 + 224.0), (1024.0, -15361.0), (-1025.0, 15360.0), (4096.0, -12288.0)]):
        ts(B("COL", j, j + 1), cq if j == 3 else ci, m, a, A.mult, A.add, ["KF"], ["COL%d" % j])
    ts(B("W1B"), B("BD"), cg, None, A.is_equal, None, ["BD", "KF"], ["W1B"])
    quant("W1Q", "W1S", "W1B", 128, ["W1B"])
    quant("UQ", "US", "UB", 128, ["UB"])
    op("v", lambda: V.tensor_copy(B("UU").bitcast(dt.uint32), B("UQ").bitcast(dt.uint32).indirect(B("OFU"))), ["UQ", "OFU"], ["UU"])
    act(B("UV"), B("US").indirect(B("OFU")), AF.Copy, ["UQ", "OFU"], ["UV"])
    dma("y", B("WQ").bitcast(dt.uint8), T.wc[:, :], "lwc", 16, ["UQ"], ["WQ"])
    dma("y", B("WP"), T.ws[:, :], "lws", 16, [], ["WP"])
    dma("y", B("VB"), T.v[:, :], "lv", 16, [], ["VB"])

    partners = [T.cores[rank ^ (1 << t)] for t in range(ROUNDS)]
    masks = [topo.mask(core, d) for d in partners]
    ne = [len(topo.engines(core, d)) for d in partners]
    sent = [0]

    def send(t, out, in_, sem, val, rd, wr):
        before("g", rd, [])
        rid, pid = topo.addr(partners[t], core)
        g.remote_dma(out, in_, T.sem[sem], T.sem.sent, pid, rid, masks[t])
        sent[0] += ne[t]
        for k in wr:
            wrote[k] = ("r", (sem, val, {}))

    def pack(t, h):
        a, z = PIECES[h]
        quant("TQ%d" % t, "TS%d" % t, "TD%d" % t, z - a, xkeys(t, h), a, "TQ%dh%d" % (t, h))

    pack(0, 0)
    pack(0, 1)
    (_, m0), (m1, _) = PIECES
    for t in range(ROUNDS):
        X, tq, tsc, lo, lr, rq, rp = ["%s%d" % (n, t) for n in ("TD", "TQ", "TS", "LO", "LR", "RQ", "RP")]
        tk = [tq + "h0", tq + "h1"]
        xk = xkeys(t, 0) + xkeys(t, 1)
        dk = [X + "d%d" % b for b in range(4)]
        last = t == ROUNDS - 1
        send(t, B(rq).bitcast(dt.uint8), B(tq).bitcast(dt.uint8), "ad%d" % t, 2 * ne[t], tk, [rq])
        send(t, B(rp), B(tsc), "ad%d" % t, 2 * ne[t], tk, [rp])
        mm("RB0", m0, B("UU", 0, 128), B("UV", 0, 128), B(tq, 0, m0), B(tsc, 0, m0), True, True, ["UU", "UV", tk[0]])
        mm("PB", C, B("UU", 0, 128), B("UV", 0, 128), B(tq), B(tsc), True, True, ["UU", "UV"] + tk)
        mm("RB1", C, B("UU", 0, 128), B("UV", 0, 128), B(tq), B(tsc), True, True, ["UU", "UV"] + tk)
        mm("NB", C, B("UU", 128, 256), B("UV", 128, 256), B(tq), B(tsc), True, True, ["UU", "UV"] + tk)
        if t == 0:
            iota("PL", [[1, C]], 0, 0)
            iota("N4", [[4, C]], 0, 0)
            iota("Q5", [[1, C]], 512, 0)
            iota("C4", [[0, 88], [1, 4]], 0, 0)
            iota("NV", [[4, C]], 4 * C, 0)
        for h, bank in enumerate(("RB0", "PB")):
            a, z = PIECES[h]
            tt(B("DM", a, z), B(bank, a, z), B("MK", a, z), A.add, [bank, "MK"], ["DM%d" % h])
            scan(B("PX", a, z), B("D0", a, z), B("DM", a, z), -1e29, A.min, A.max, ["D0", "DM%d" % h], ["PX%d" % h])
        for k in ON_S:
            n = 16 * k
            act(B("DR", 0, n), B("RB1", 0, n), AF.Relu, ["RB1", "PX0", "PX1"], ["DR"], bias=B("PX", n + 15, n + 16), scale=-1.0)
            m, b = [(m, ks.index(k)) for m, (w, ks) in enumerate(SLOTS) if k in ks][0]
            act(B("G%d" % m, b, 4 * n, 4), B("DR", 0, n), AF.Sign, ["DR"], ["G%d.%d" % (m, b), "RS%d" % k], scale=-1.0,
                accum_out=B("RS", k, k + 1))
        queue = []

        def flush(m):
            w = SLOTS[m][0]
            quant("GQ%d" % m, "GS%d" % m, "G%d" % m, w, ["G%d.%d" % (m, b) for b in range(4)])
            mm("CS", w, B("W1Q"), B("W1S"), B("GQ%d" % m), B("GS%d" % m), m == 0, m == len(SLOTS) - 1, ["W1Q", "GQ%d" % m])

        for m, (w, ks) in enumerate(SLOTS):
            for b, k in enumerate(ks):
                gk = "G%d.%d" % (m, b)
                if k == 0:
                    tt(B("G0", 0, 4 * C, 4), B("PB", 0, C), B("PX"), A.is_gt, ["PB", "PX0", "PX1"], [gk])
                elif k not in ON_S:
                    n = 16 * k
                    ts(B("G%d" % m, b, 4 * n, 4), B("PB", 0, n), B("PX", n + 15, n + 16), None, A.is_ge, None, ["PB", "PX0", "PX1"], [gk])
                    act(B("JUNK", 8 * k * (k - 1), 8 * k * (k + 1)), B("G%d" % m, b, 4 * n, 4), AF.Copy, [gk], ["J%d" % k, "RS%d" % k],
                        accum_out=B("RS", k, k + 1))
                if b == 0 and queue:
                    flush(queue.pop())
            queue.append(m)
        if t == 0:
            op("v", lambda: V.memset(B("RS", 0, 1), 0.0), [], ["RS0"])
        flush(queue.pop())
        scan(B("DS"), B("RST"), B("G0", 0, 4 * C, 4), 0.0, A.mult, A.add, ["RST", "G0.0"], ["DS"])
        if t == 0:
            ts(B("CW"), B("CWI"), B("COL", 2, 3), None, A.add, None, ["CWI", "COL2"], ["CW"])
            for k in ON_S:
                ts(B("CW", k, k + 1), B("CW", k, k + 1), float(16 * k), None, A.add, None, ["CW"], ["CW"])
            for k in sorted(ON_S):
                ts(B("CW", k, 22), B("CW", k, 22), 16.0, None, A.add, None, ["CW"], ["CW"])
            tt(B("COL", 4, 5), B("COL", 3, 4), cr, A.add, ["COL3", "KF"], ["COL4"])
        act(B("SGN"), B("NB", 0, C), AF.Sign, ["NB"], ["SGN"])
        act(B("SGP"), B("SGN"), AF.Relu, ["SGN"], ["SGP", "NC"], accum_out=B("NC", 0, 1))
        act(B("WC1", 0, 1), B("NC", 0, 1), AF.Relu, ["NC"], ["WC1"], bias=224.0, scale=-1.0)
        act(B("BC", 0, 1), B("WC1", 0, 1), AF.Copy, ["WC1"], ["BC"], bias=-287.5)
        act(B("SC", 0, 1), B("WC1", 0, 1), AF.Identity, ["WC1", "COL0"], ["SC"], bias=B("COL", 0, 1), scale=-1.0)
        act(B("SQ"), B("PL"), AF.Square, ["PL", "BC"], ["SQ"], bias=B("BC", 0, 1))
        act(B("SG2"), B("SQ"), AF.Sign, ["SQ"], ["SG2"], bias=4096.0, scale=-1.0)
        tt(B("TA"), B("CW"), B("DS", 15, C, 16), A.add, ["CW", "DS"], ["TA"])
        tt(B("TB"), B("TA"), B("RS"), A.add, ["TA"] + ["RS%d" % k for k in range(22)], ["TB"])
        scan(B("PKX"), B("PKA"), B("CS", 0, C), 0.0, A.add, A.max, ["PKA", "CS"], ["PKX"])
        tt(B("RF"), B("TB"), B("PKX", 15, C, 16), A.subtract, ["TB", "PKX"], ["RF"])
        cp(B(lo), B("RF"), ["RF"], [lo])
        send(t, B(lr), B(lo), "al%d" % t, ne[t], [lo], [lr])
        act(B("NKR"), B("SG2").indirect(B(lo)), AF.Relu, ["SG2", lo], ["NKR"], scale=-1.0)
        op("v", lambda: V.tensor_copy(B("HW").indirect(B(lo)), B("N4")), ["N4", lo], ["HW"])
        tt(B("RKR"), B("SG2").indirect(B(lo)), B("Q5"), A.mult, ["SG2", lo, "Q5"], ["RKR"])
        if t == 0:
            for b in range(4):
                ze, at = "ZE%d" % (b % 2), 2 + b % 2 - b
                op("v", (lambda b=b, ze=ze, at=at: V.quantize_mx(B("EQ%d" % b), B("ES%d" % b), B(ze, at, at + 512))), [ze], ["EQ%d" % b])
        if t == 1:
            quant("VQ", "VS", "VB", 128, ["VB"])
        for b in range(4):
            mm("RB%d" % b, C, B("EQ%d" % b), B("ES%d" % b), B(rq), B(rp), True, True, ["EQ%d" % b, rq, rp])
        for b in range(4):
            act(B(X, 4 * C + b, 8 * C, 4), B("RB%d" % b, 0, C), AF.Copy, ["RB%d" % b], [dk[b]])
        if t == 0:
            act(B("D4"), B("C4"), AF.Abs, ["C4", "KF"], ["D4"], bias=cq, scale=-1.0)
            act(B("NE4"), B("D4"), AF.Sign, ["D4"], ["NE4"])
            act(B("PKB"), B("NE4"), AF.Copy, ["NE4"], ["PKB"], bias=-262144.0, scale=262144.0 + 4096.0)
        op("v", lambda: V.tensor_copy(B("KP").indirect(B(lr)), B("NKR")), ["NKR", lr], ["KP"])
        scan(B("E1"), B("KP"), B("KP"), 0.0, A.add, A.max, ["KP"], ["E1"])
        tt(B("GX"), B("E1").indirect(B(lr)), B("RKR"), A.max, ["E1", lr, "RKR"], ["GX"])
        scan(B("GP"), B("PKA"), B("GX"), 0.0, A.add, A.max, ["PKA", "GX"], ["GP"])
        gp = B("GP", 15, C, 16)
        ts(B("MM"), gp, B("SC", 0, 1), 128.0, A.is_gt, A.mult, ["GP", "SC"], ["MM"])
        tt(B("DD"), gp, B("MM"), A.add, ["GP", "MM"], ["DD"])
        ts(B("DST"), B("DD"), B("COL", 1, 2), None, A.add, None, ["DD", "COL1"], ["DST"])
        op("v", lambda: V.tensor_copy(B("HW").indirect(B("DST")), B("NV")), ["NV", "DST"], ["HW"])
        scan(B("HP"), B("PKB"), B("HW", 0, C), 0.0, A.add, A.max, ["PKB", "HW"], ["HP"])
        ts(B("L2"), B("HP", 3, C, 4), B("COL", 4, 5), None, A.add, None, ["HP", "COL4"], ["L2"])
        if last:
            act(B("HS"), B("HW", 0, C), AF.Sign, ["HW"], ["HS"], bias=-1407.0)
        ts(B("FT", 0, 4 * m0), B(X).indirect(B("L2", 0, m0 // 4)), 0.015625, None, A.mult, None, xk + dk + ["L2"], ["FT0"])
        act(B("FT", 4 * m1, 4 * C), B(X).indirect(B("L2", m1 // 4, 88)), AF.Copy, xk + dk + ["L2"], ["FT1"], scale=0.015625)
        quant("FQ", "FS", "FT", m0, ["FT0"], 0, "FQ0")
        ts(B("FF", 0, 4 * m0), B("FT", 0, 4 * m0), 64.0, None, A.mult, None, ["FT0"], ["FF0"])
        act(B("FF", 4 * m1, 4 * C), B("FT", 4 * m1, 4 * C), AF.Copy, ["FT1"], ["FF1"], scale=64.0)
        if last:
            act(B("HQ"), B("HW", 0, C), AF.Copy, ["HW"], ["HQ"], bias=-176.0, scale=0.25)
            act(B("HT"), B("HS"), AF.Copy, ["HS"], ["HT"], scale=-176.0)
        Y = "TD%d" % (t + 1)
        for h, (a, z) in enumerate(PIECES):
            for b in range(4):
                bank = BANKS[h][b]
                mm(bank, z - a, B("WQ", 128 * b, 128 * b + 128), B("WP", 128 * b, 128 * b + 128), B("FQ", a, z), B("FS", a, z),
                   True, True, ["WQ", "WP", "FQ%d" % h])
                tt(B(Y, 4 * a + b, 4 * z, 4), B(bank, 0, z - a), B("FF", 4 * a + b, 4 * z, 4), A.add, [bank, "FF%d" % h], [Y + "x%d%d" % (h, b)])
                if (h, b) == (0, QAT):
                    quant("FQ", "FS", "FT", C - m1, ["FT1"], m1, "FQ1")
            pack(t + 1, h)

    stores = []

    def store(q, out, in_, rd):
        before(q, rd, [])
        stores.append("od" if q == "y" else "os")
        eng[q].dma_start(out, in_).then_inc(T.sem[stores[-1]], 16)

    for h, (a, z) in enumerate(PIECES):
        mm("RB%d" % h, z - a, B("VQ"), B("VS"), B("TQ3", a, z), B("TS3", a, z), True, True, ["VQ", "TQ3h%d" % h])
        store("y", T.oc[:, 4 * a:4 * z], B("TQ3", a, z).bitcast(dt.uint8), ["TQ3h%d" % h])
        act(B("YB", a, z), B("RB%d" % h, 0, z - a), AF.Copy, ["RB%d" % h], ["YB%d" % h])
        store("s", T.y[:, a:z], B("YB", a, z), ["YB%d" % h])
    tt(B("HO"), B("HQ"), B("HT"), A.add, ["HQ", "HT"], ["HO"])
    for k in range(4):
        store("y", T.osc[4 * k:4 * k + 4, :], T.TS3[32 * k:32 * k + 4, :], ["TQ3h0", "TQ3h1"])
    store("s", T.ot[:, :], T.HO[0:128:16, :], ["HO"])
    g.wait_ge(T.sem.sent, sent[0])
    for q in ("v", "s", "p", "g"):
        g.wait_ge(T.sem["c" + q], count[q])
    g.wait_ge(T.sem.od, 16 * stores.count("od"))
    g.wait_ge(T.sem["os"], 16 * stores.count("os"))
